import numpy as np
import ml_dtypes


def mxq(x, axis, fmt="e4m3"):
    dtype, down = {"e4m3": (ml_dtypes.float8_e4m3fn, 7), "e5m2": (ml_dtypes.float8_e5m2, 14)}[fmt]
    v = np.moveaxis(np.asarray(x, np.float32).astype(ml_dtypes.bfloat16).astype(np.float64), axis, -1)
    blocks = v.reshape(v.shape[:-1] + (-1, 32))
    amax = np.abs(blocks).max(-1, keepdims=True)
    byte = np.maximum(np.where(amax > 0, np.frexp(amax)[1] - 1 + 127, 0) - down, 1)
    scale = np.exp2(byte - 127.0)
    codes = (blocks / scale).astype(np.float32).astype(dtype).astype(np.float64)
    return np.moveaxis((codes * scale).reshape(v.shape), -1, axis)


WIDE = False


def mx_kscale(k):
    if not WIDE:
        return np.ones(k)
    levels = np.array([10, -10, 5, -5, 0])
    if k % 512:
        return np.exp2(np.random.permutation(np.resize(levels, k // 32))).repeat(32)
    a = np.empty((k // 512, 16))
    for p in range(k // 512):
        a[p, :8] = np.random.permutation(np.resize(levels, 8))
        for g in range(8):
            far = levels[np.abs(levels - a[p, g]) >= 10]
            a[p, g + 8] = far[np.random.randint(len(far))]
    return np.exp2(a.ravel()).repeat(32)


BF16 = ml_dtypes.bfloat16


def bf(x):
    return np.asarray(x, np.float32).astype(BF16)


def f64(x):
    return np.asarray(x).astype(np.float64)


E2M1 = np.array([0.0, 0.5, 1.0, 1.5, 2.0, 3.0, 4.0, 6.0, -0.0, -0.5, -1.0, -1.5, -2.0, -3.0, -4.0, -6.0])


def pack_weight(w, fmt):
    k, n = w.shape
    w = f64(bf(w)).reshape(k // 32, 32, n)
    amax = np.abs(w).max(1)
    if fmt == "e4m3":
        byte = np.frexp(amax)[1] - 1 + 127 - 7
    else:
        mant, ex = np.frexp(amax / 6.0)
        byte = np.where(mant > 0.5, ex, ex - 1) + 127
    byte = np.clip(np.where(amax > 0, byte, 1), 1, 254)
    scaled = (w * np.exp2(127.0 - byte)[:, None, :]).reshape(k, n).astype(np.float32)
    by_word = np.ascontiguousarray(scaled.reshape(k // 512, 128, 4, n).transpose(0, 1, 3, 2))
    if fmt == "e4m3":
        words = by_word.astype(ml_dtypes.float8_e4m3fn).view(np.uint8)
    else:
        c = by_word.astype(ml_dtypes.float4_e2m1fn).view(np.uint8) & 0xF
        words = c[..., 0::2] | (c[..., 1::2] << 4)
    return np.ascontiguousarray(words), np.ascontiguousarray(byte.astype(np.uint8).reshape(k // 512, 16, n))


def unpack_weight(words, scales, fmt):
    g, p, n, _ = words.shape
    if fmt == "e4m3":
        vals = np.ascontiguousarray(words).view(ml_dtypes.float8_e4m3fn).astype(np.float64)
    else:
        nib = np.empty((g, p, n, 4), np.uint8)
        nib[..., 0::2] = words & 0xF
        nib[..., 1::2] = words >> 4
        vals = E2M1[nib]
    vals = vals * np.repeat(np.exp2(scales.astype(np.float64) - 127.0), 8, axis=1)[..., None]
    return vals.transpose(0, 1, 3, 2).reshape(g * 512, n)
def pack4(w):
    words, scales = pack_weight(w, "e2m1")
    return words.reshape(words.shape[0], 128, -1), scales


def unpack4(words, scales):
    return unpack_weight(words.reshape(words.shape[0], 128, -1, 2), scales, "e2m1")


M, KA, KB, N = 2048, 512, 1536, 1024

MISSING = 0.75
DAMP = 0.75


def setup_inputs():
    s, t = mx_kscale(KA), mx_kscale(KB)
    units = np.concatenate([s, t])
    mean = 0.5 * np.random.standard_normal(KA + KB)
    x = mean + np.random.standard_normal((M, KA + KB))
    pa = np.random.standard_normal((KA, N)) / np.sqrt(2 * KA)
    pb = np.random.standard_normal((KB, N)) / np.sqrt(2 * KB)
    pb_words, pb_scales = pack4(pb / t[:, None])
    return {"x": bf(x * units),
            "mu": bf(mean * units),
            "pa": bf(pa / s[:, None]),
            "pb_words": pb_words,
            "pb_scales": pb_scales,
            "dinv": bf(1 + 0.1 * np.random.standard_normal(N)),
            "y": bf(np.random.standard_normal((M, N))),
            "step": bf(DAMP * (np.random.random((M, N)) < MISSING))}


def reference(x, mu, pa, pb_words, pb_scales, dinv, y, step):
    c = f64(x) - f64(mu)
    ca = mxq(c[:, :KA], 1, "e4m3")
    cb = mxq(c[:, KA:], 1, "e4m3")
    wa = mxq(f64(pa), 0, "e4m3")
    wb = unpack4(pb_words, pb_scales)
    r = (ca @ wa) + (cb @ wb)
    residual = f64(y) + r * f64(dinv)
    return f64(y) - f64(step) * residual

@@ -1,0 +1,264 @@
+from contextlib import ExitStack
+
+import concourse.mybir as mybir
+from concourse.masks import make_identity
+
+M, KA, KB, N = 2048, 512, 1536, 1024
+K = KA + KB
+FLOPS = 2 * M * K * N
+
+F32 = mybir.dt.float32
+BF16 = mybir.dt.bfloat16
+U32 = mybir.dt.uint32
+I32 = mybir.dt.int32
+U8 = mybir.dt.uint8
+E4M3X4 = mybir.dt.float8_e4m3fn_x4
+E2M1X4 = mybir.dt.float4_e2m1fn_x4
+ALU = mybir.AluOpType
+ACT = mybir.ActivationFunctionType
+
+P = 128
+G = K // 512
+ROWS = 512
+NG = M // ROWS
+TILES = ROWS // P
+NB = N // P
+HALF = 512
+SLOTS = NG * 4
+
+
+def tile_gaussian_imputation_jacobi_s1_kernel(tc, x, mu, pa, pb_words, pb_scales, dinv, y, step, out):
+    nc = tc.nc
+    with ExitStack() as ctx:
+        keep = ctx.enter_context(tc.tile_pool(name="keep", bufs=1))
+        work = ctx.enter_context(tc.tile_pool(name="work", bufs=2))
+        psum = ctx.enter_context(tc.psum_pool(name="psum", bufs=1))
+        ctx.enter_context(nc.allow_non_contiguous_dma(reason="mu lies 4 values a partition"))
+        ctx.enter_context(tc.manual_schedule())
+
+        ident_f = keep.tile([P, P], F32, name="ident_f")
+        ident_b = keep.tile([P, P], BF16, name="ident_b")
+        mu_t = keep.tile([P, G, 4], BF16, name="mu_t", align_bytes=64)
+        dinv_rows = keep.tile([P, P], BF16, name="dinv_rows")
+        dinv_t = keep.tile([P, NB], F32, name="dinv_t")
+        warm = keep.tile([P, 1], F32, name="warm")
+        pa_raw = keep.tile([P, 4, N], BF16, name="pa_raw", align_bytes=64)
+        pa_grp = keep.tile([P, N, 4], BF16, name="pa_grp", align_bytes=64)
+        pa_codes = keep.tile([P, N], U32, name="pa_codes", align_bytes=64)
+        pa_scale = keep.tile([P, N], U8, name="pa_scale", align_bytes=64)
+        pb_codes = keep.tile([P, G - 1, 2 * N], U8, name="pb_codes", align_bytes=64)
+        pb_scale = keep.tile([P, G - 1, N], U8, name="pb_scale", align_bytes=64)
+
+        x_tiles, xp_tiles, step_tiles, y_tiles = {}, {}, {}, {}
+        codes, scales, xts, xcs = {}, {}, {}, {}
+        sts, step_ts, accs, vs, a_tiles, w_tiles = {}, {}, {}, {}, {}, {}
+
+        def load_x(t):
+            x_tiles[t] = work.tile([P, K], BF16, name="x_in", tag="x_in", bufs=6, align_bytes=64)
+            nc.sync.dma_start(out=x_tiles[t][:], in_=x[t * P : (t + 1) * P, :])
+
+        def load_rows(store, src, g, name):
+            store[g] = work.tile([P, TILES, N], BF16, name=name, tag=name, bufs=2, align_bytes=64)
+            nc.sync.dma_start(out=store[g][:], in_=src[g * ROWS : (g + 1) * ROWS, :].rearrange("(i p) n -> p i n", p=P))
+
+        def permute(t):
+            xp_tiles[t] = work.tile([P, G, 2, P], F32, name="xp", tag="xp", bufs=6, align_bytes=64)
+            nc.scalar.copy(
+                out=xp_tiles[t][:],
+                in_=x_tiles[t][:].bitcast(F32).rearrange("r (g p u) -> r g u p", p=P, u=2),
+            )
+
+        def turn_x(h, j, gp):
+            for gi in range(2):
+                xt = psum.tile([P, 2, 256], F32, name="xt%d" % gi, tag="xt%d" % gi, bufs=1)
+                for i in range(2):
+                    for u in range(2):
+                        nc.tensor.transpose(
+                            xt[:, u, i * P : (i + 1) * P], xp_tiles[h * TILES + 2 * j + i][:, 2 * gp + gi, u, :], ident_f[:]
+                        )
+                xts[(h, j, gp, gi)] = xt
+
+        def centre(h, j, gp):
+            xc = work.tile([P, 2, 256, 4], BF16, name="xc", tag="xc", bufs=3, align_bytes=64)
+            for gi in range(2):
+                g = 2 * gp + gi
+                nc.vector.tensor_tensor(
+                    out=xc[:, gi].rearrange("p r (u e) -> p r u e", e=2),
+                    in0=xts[(h, j, gp, gi)][:].bitcast(BF16).rearrange("p u (r e) -> p r u e", e=2),
+                    in1=mu_t[:, g, :].rearrange("p (u e) -> p u e", e=2).unsqueeze(1).to_broadcast([P, 256, 2, 2]),
+                    op=ALU.subtract,
+                )
+            xcs[(h, j, gp)] = xc
+
+        def quantise(h, j, gp, gi):
+            if h not in codes:
+                codes[h] = work.tile([P, G, ROWS], U32, name="codes", tag="codes", bufs=2, align_bytes=64)
+                scales[h] = work.tile([P, G, ROWS], U8, name="scales", tag="scales", bufs=2, align_bytes=64)
+            g = 2 * gp + gi
+            nc.vector.quantize_mx(
+                out=codes[h][:, g, 256 * j : 256 * (j + 1)].bitcast(E4M3X4),
+                scales=scales[h][:, g, 256 * j : 256 * (j + 1)],
+                in_=xcs[(h, j, gp)][:, gi].rearrange("p r t -> p (r t)"),
+            )
+
+        def turn_step(s):
+            g, q = divmod(s, 4)
+            st = psum.tile([P, 2, ROWS], BF16, name="st", tag="st", bufs=1)
+            for k in range(2):
+                for i in range(TILES):
+                    nc.tensor.transpose(
+                        st[:, k, i * P : (i + 1) * P], step_tiles[g][:, i, (2 * q + k) * P : (2 * q + k + 1) * P], ident_b[:]
+                    )
+            step_ts[s] = work.tile([P, 2, ROWS], BF16, name="step_t", tag="step_t", bufs=3, align_bytes=64)
+            nc.scalar.copy(out=step_ts[s][:], in_=st[:])
+
+        def multiply(g, nb):
+            acc = psum.tile([P, ROWS], F32, name="acc", tag="acc", bufs=3)
+            cols = slice(nb * P, (nb + 1) * P)
+            order = (1, 2, 3, 0)
+            for n, k in enumerate(order):
+                if k == 0:
+                    w, ws = pa_codes[:, cols].bitcast(E4M3X4), pa_scale[:, cols]
+                else:
+                    w = pb_codes[:, k - 1, 2 * nb * P : 2 * (nb + 1) * P].bitcast(E2M1X4)
+                    ws = pb_scale[:, k - 1, cols]
+                nc.tensor.matmul_mx(
+                    out=acc[:],
+                    lhsT=w,
+                    lhsT_scale=ws,
+                    rhs=codes[g][:, k, :].bitcast(E4M3X4),
+                    rhs_scale=scales[g][:, k, :],
+                    start=(n == 0),
+                    stop=(n == G - 1),
+                )
+            accs[(g, nb)] = acc
+
+        def damp(g, nb):
+            v = work.tile([P, ROWS], F32, name="v", tag="v", bufs=12, align_bytes=64)
+            nc.vector.scalar_tensor_tensor(
+                out=v[:],
+                in0=accs[(g, nb)][:],
+                scalar=dinv_t[:, nb : nb + 1],
+                in1=step_ts[4 * g + nb // 2][:, nb % 2, :],
+                op0=ALU.mult,
+                op1=ALU.mult,
+            )
+            vs[(g, nb)] = v
+
+        def keep_part(g, h, i):
+            cols = slice(h * HALF, (h + 1) * HALF)
+            w = work.tile([P, HALF], F32, name="w", tag="w", bufs=3, align_bytes=64)
+            nc.scalar.activation(out=w[:], in_=step_tiles[g][:, i, cols], func=ACT.Identity, bias=1.0, scale=-1.0)
+            a = work.tile([P, HALF], F32, name="a", tag="a", bufs=5, align_bytes=64)
+            nc.gpsimd.tensor_tensor(out=a[:], in0=w[:], in1=y_tiles[g][:, i, cols], op=ALU.mult)
+            a_tiles[(g, h, i)] = a
+
+        def finish(g, h, i):
+            vb = psum.tile([P, 4, P], F32, name="vb", tag="vb", bufs=2)
+            for c in range(4):
+                nc.tensor.transpose(vb[:, c, :], vs[(g, 4 * h + c)][:, i * P : (i + 1) * P], ident_f[:])
+            o = work.tile([P, HALF], F32, name="o", tag="o", bufs=6, align_bytes=64)
+            nc.vector.tensor_tensor(
+                out=o[:], in0=a_tiles[(g, h, i)][:], in1=vb[:].rearrange("p c n -> p (c n)"), op=ALU.subtract
+            )
+            r0 = g * ROWS + i * P
+            nc.sync.dma_start(out=out[r0 : r0 + P, h * HALF : (h + 1) * HALF], in_=o[:])
+
+        def finish_units(s):
+            n = 2 * (s - 2)
+            if n < 0 or n >= NG * 8:
+                return []
+            return [(m // 8, (m % 8) // 4, m % 4) for m in (n, n + 1)]
+
+        def group_pa(c, engine):
+            cols = slice(c * 256, (c + 1) * 256)
+            dst, src = pa_grp[:, cols, :], pa_raw[:, :, cols].rearrange("p j n -> p n j")
+            if engine == 0:
+                nc.vector.tensor_copy(out=dst, in_=src)
+            else:
+                nc.scalar.copy(out=dst, in_=src)
+
+        def quantise_pa(c):
+            cols = slice(c * 256, (c + 1) * 256)
+            nc.vector.quantize_mx(
+                out=pa_codes[:, cols].bitcast(E4M3X4),
+                scales=pa_scale[:, cols],
+                in_=pa_grp[:, cols, :].rearrange("p n j -> p (n j)"),
+            )
+
+        for t in range(4):
+            load_x(t)
+        nc.vector.memset(pb_scale[:].rearrange("p g n -> p (g n)").bitcast(I32), 0)
+        nc.vector.memset(dinv_rows[:], 0.0)
+        nc.vector.memset(warm[:], 0.0)
+        nc.scalar.dma_start(out=mu_t[:], in_=mu.rearrange("(g p t) -> p g t", p=P, t=4))
+        nc.scalar.dma_start(out=dinv_rows[0:NB, :], in_=dinv.rearrange("(b p) -> b p", p=P))
+        for q in range(4):
+            nc.scalar.dma_start(
+                out=pb_scale[32 * q : 32 * q + 4, :, :].bitcast(I32),
+                in_=pb_scales[:, 4 * q : 4 * q + 4, :].rearrange("g r n -> r g n").bitcast(I32),
+            )
+        nc.scalar.activation(out=warm[:], in_=warm[:], func=ACT.Identity, bias=0.0, scale=1.0)
+        make_identity(nc, ident_f[:])
+        make_identity(nc, ident_b[:])
+        nc.sync.dma_start(
+            out=pb_codes[:].bitcast(I32), in_=pb_words.rearrange("g p b -> p g b").bitcast(I32)
+        )
+        nc.sync.dma_start(out=pa_raw[:], in_=pa.rearrange("(p j) n -> p j n", j=4))
+        load_rows(step_tiles, step, 0, "step_in")
+        load_x(4)
+        load_x(5)
+        load_rows(y_tiles, y, 0, "y_in")
+        load_x(6)
+        load_x(7)
+
+        dt = psum.tile([P, P], BF16, name="dt", tag="st", bufs=1)
+        nc.tensor.transpose(dt[:], dinv_rows[:], ident_b[:])
+        nc.vector.tensor_copy(out=dinv_t[:], in_=dt[:, 0:NB])
+
+        for j in range(2):
+            permute(2 * j)
+            permute(2 * j + 1)
+            for gp in range(2):
+                turn_x(0, j, gp)
+                centre(0, j, gp)
+            for gp in range(2):
+                for gi in range(2):
+                    quantise(0, j, gp, gi)
+        group_pa(0, 0)
+        for c in range(1, 4):
+            group_pa(c, 1)
+        permute(4)
+        permute(5)
+        quantise_pa(0)
+
+        for s in range(SLOTS + 2):
+            g, q = divmod(s, 4)
+            ahead = s < SLOTS and g + 1 < NG
+            if s + 8 < M // P and s < SLOTS:
+                load_x(s + 8)
+            if s < SLOTS and q == 1 and g + 1 < NG:
+                load_rows(step_tiles, step, g + 1, "step_in")
+            if s < SLOTS and q == 2 and g + 1 < NG:
+                load_rows(y_tiles, y, g + 1, "y_in")
+            if s + 6 < M // P:
+                permute(s + 6)
+            j, gp = divmod(q, 2)
+            if ahead:
+                turn_x(g + 1, j, gp)
+                centre(g + 1, j, gp)
+            if s < SLOTS:
+                turn_step(s)
+            for unit in finish_units(s):
+                finish(*unit)
+            for unit in finish_units(s + 1):
+                keep_part(*unit)
+            if s == SLOTS + 1 or s >= SLOTS:
+                continue
+            if s + 1 < 4:
+                quantise_pa(s + 1)
+            for k in range(2):
+                if ahead:
+                    quantise(g + 1, j, gp, k)
+                multiply(g, 2 * q + k)
+                damp(g, 2 * q + k)

@@ -5,6 +5,7 @@ from concourse.masks import make_identity
 
 M, KA, KB, N = 2048, 512, 1536, 1024
 K = KA + KB
+ABUFS = 2
 FLOPS = 2 * M * K * N
 
 F32 = mybir.dt.float32
@@ -25,6 +26,7 @@ TILES = ROWS // P
 NB = N // P
 HALF = 512
 SLOTS = NG * 4
+FINISHED = {12: 3, 13: 3, 14: 3, 15: 1, 16: 4}
 
 
 def tile_gaussian_imputation_jacobi_s1_kernel(tc, x, mu, pa, pb_words, pb_scales, dinv, y, step, out):
@@ -51,7 +53,7 @@ def tile_gaussian_imputation_jacobi_s1_kernel(tc, x, mu, pa, pb_words, pb_scales
 
         x_tiles, xp_tiles, step_tiles, y_tiles = {}, {}, {}, {}
         codes, scales, xts, xcs = {}, {}, {}, {}
-        sts, step_ts, accs, vs, a_tiles, w_tiles = {}, {}, {}, {}, {}, {}
+        vbs, step_ts, accs, vs, a_tiles, w_tiles = {}, {}, {}, {}, {}, {}
 
         def load_x(t):
             x_tiles[t] = work.tile([P, K], BF16, name="x_in", tag="x_in", bufs=6, align_bytes=64)
@@ -68,9 +70,18 @@ def tile_gaussian_imputation_jacobi_s1_kernel(tc, x, mu, pa, pb_words, pb_scales
                 in_=x_tiles[t][:].bitcast(F32).rearrange("r (g p u) -> r g u p", p=P, u=2),
             )
 
-        def turn_x(h, j, gp):
+        def turn_x_words(j, gp, tag):
             for gi in range(2):
-                xt = psum.tile([P, 2, 256], F32, name="xt%d" % gi, tag="xt%d" % gi, bufs=1)
+                xt = psum.tile([P, 2, 256], F32, name="xt", tag=tag, bufs=2)
+                for i in range(2):
+                    words = x_tiles[2 * j + i][:].bitcast(F32).rearrange("r (g p u) -> r g u p", p=P, u=2)
+                    for u in range(2):
+                        nc.tensor.transpose(xt[:, u, i * P : (i + 1) * P], words[:, 2 * gp + gi, u, :], ident_f[:])
+                xts[(0, j, gp, gi)] = xt
+
+        def turn_x(h, j, gp, tag="xt"):
+            for gi in range(2):
+                xt = psum.tile([P, 2, 256], F32, name="xt", tag=tag, bufs=2)
                 for i in range(2):
                     for u in range(2):
                         nc.tensor.transpose(
@@ -134,7 +145,7 @@ def tile_gaussian_imputation_jacobi_s1_kernel(tc, x, mu, pa, pb_words, pb_scales
             accs[(g, nb)] = acc
 
         def damp(g, nb):
-            v = work.tile([P, ROWS], F32, name="v", tag="v", bufs=12, align_bytes=64)
+            v = work.tile([P, ROWS], F32, name="v", tag="v", bufs=14, align_bytes=64)
             nc.vector.scalar_tensor_tensor(
                 out=v[:],
                 in0=accs[(g, nb)][:],
@@ -147,16 +158,20 @@ def tile_gaussian_imputation_jacobi_s1_kernel(tc, x, mu, pa, pb_words, pb_scales
 
         def keep_part(g, h, i):
             cols = slice(h * HALF, (h + 1) * HALF)
-            w = work.tile([P, HALF], F32, name="w", tag="w", bufs=3, align_bytes=64)
+            w = work.tile([P, HALF], F32, name="w", tag="w", bufs=4, align_bytes=64)
             nc.scalar.activation(out=w[:], in_=step_tiles[g][:, i, cols], func=ACT.Identity, bias=1.0, scale=-1.0)
-            a = work.tile([P, HALF], F32, name="a", tag="a", bufs=5, align_bytes=64)
+            a = work.tile([P, HALF], F32, name="a", tag="a", bufs=ABUFS, align_bytes=64)
             nc.gpsimd.tensor_tensor(out=a[:], in0=w[:], in1=y_tiles[g][:, i, cols], op=ALU.mult)
             a_tiles[(g, h, i)] = a
 
-        def finish(g, h, i):
-            vb = psum.tile([P, 4, P], F32, name="vb", tag="vb", bufs=2)
+        def turn_back(g, h, i, tag="vb"):
+            vb = psum.tile([P, 4, P], F32, name="vb", tag=tag, bufs=2)
             for c in range(4):
                 nc.tensor.transpose(vb[:, c, :], vs[(g, 4 * h + c)][:, i * P : (i + 1) * P], ident_f[:])
+            vbs[(g, h, i)] = vb
+
+        def finish(g, h, i):
+            vb = vbs[(g, h, i)]
             o = work.tile([P, HALF], F32, name="o", tag="o", bufs=6, align_bytes=64)
             nc.vector.tensor_tensor(
                 out=o[:], in0=a_tiles[(g, h, i)][:], in1=vb[:].rearrange("p c n -> p (c n)"), op=ALU.subtract
@@ -164,11 +179,14 @@ def tile_gaussian_imputation_jacobi_s1_kernel(tc, x, mu, pa, pb_words, pb_scales
             r0 = g * ROWS + i * P
             nc.sync.dma_start(out=out[r0 : r0 + P, h * HALF : (h + 1) * HALF], in_=o[:])
 
+        first_unit = [0] * (SLOTS + 2)
+        for s in range(SLOTS + 1):
+            first_unit[s + 1] = first_unit[s] + FINISHED.get(s, 2 if s >= 3 else 0)
+
         def finish_units(s):
-            n = 2 * (s - 2)
-            if n < 0 or n >= NG * 8:
+            if s > SLOTS:
                 return []
-            return [(m // 8, (m % 8) // 4, m % 4) for m in (n, n + 1)]
+            return [(m // 8, (m % 8) // 4, m % 4) for m in range(first_unit[s], first_unit[s + 1])]
 
         def group_pa(c, engine):
             cols = slice(c * 256, (c + 1) * 256)
@@ -186,79 +204,99 @@ def tile_gaussian_imputation_jacobi_s1_kernel(tc, x, mu, pa, pb_words, pb_scales
                 in_=pa_grp[:, cols, :].rearrange("p n j -> p (n j)"),
             )
 
+        nc.vector.memset(warm[:], 0.0)
+        nc.vector.memset(dinv_rows[:], 0.0)
+        nc.vector.memset(pb_scale[:].rearrange("p g n -> p (g n)").bitcast(I32), 0)
         for t in range(4):
             load_x(t)
-        nc.vector.memset(pb_scale[:].rearrange("p g n -> p (g n)").bitcast(I32), 0)
-        nc.vector.memset(dinv_rows[:], 0.0)
-        nc.vector.memset(warm[:], 0.0)
         nc.scalar.dma_start(out=mu_t[:], in_=mu.rearrange("(g p t) -> p g t", p=P, t=4))
         nc.scalar.dma_start(out=dinv_rows[0:NB, :], in_=dinv.rearrange("(b p) -> b p", p=P))
-        for q in range(4):
-            nc.scalar.dma_start(
-                out=pb_scale[32 * q : 32 * q + 4, :, :].bitcast(I32),
-                in_=pb_scales[:, 4 * q : 4 * q + 4, :].rearrange("g r n -> r g n").bitcast(I32),
-            )
         nc.scalar.activation(out=warm[:], in_=warm[:], func=ACT.Identity, bias=0.0, scale=1.0)
         make_identity(nc, ident_f[:])
         make_identity(nc, ident_b[:])
         nc.sync.dma_start(
             out=pb_codes[:].bitcast(I32), in_=pb_words.rearrange("g p b -> p g b").bitcast(I32)
         )
-        nc.sync.dma_start(out=pa_raw[:], in_=pa.rearrange("(p j) n -> p j n", j=4))
-        load_rows(step_tiles, step, 0, "step_in")
-        load_x(4)
-        load_x(5)
-        load_rows(y_tiles, y, 0, "y_in")
+        for q in range(4):
+            nc.sync.dma_start(
+                out=pb_scale[32 * q : 32 * q + 4, :, :].bitcast(I32),
+                in_=pb_scales[:, 4 * q : 4 * q + 4, :].rearrange("g r n -> r g n").bitcast(I32),
+            )
+        step_tiles[0] = work.tile([P, TILES, N], BF16, name="step_in", tag="step_in", bufs=2, align_bytes=64)
+        for h in range(2):
+            cols = slice(h * HALF, (h + 1) * HALF)
+            nc.sync.dma_start(out=pa_raw[:, :, cols], in_=pa[:, cols].rearrange("(p j) n -> p j n", j=4))
+            nc.sync.dma_start(
+                out=step_tiles[0][:, :, cols], in_=step[0:ROWS, cols].rearrange("(i p) n -> p i n", p=P)
+            )
+            if h == 0:
+                load_x(4)
+                load_x(5)
         load_x(6)
         load_x(7)
-
-        dt = psum.tile([P, P], BF16, name="dt", tag="st", bufs=1)
-        nc.tensor.transpose(dt[:], dinv_rows[:], ident_b[:])
-        nc.vector.tensor_copy(out=dinv_t[:], in_=dt[:, 0:NB])
+        load_rows(y_tiles, y, 0, "y_in")
 
         for j in range(2):
-            permute(2 * j)
-            permute(2 * j + 1)
-            for gp in range(2):
-                turn_x(0, j, gp)
+            for gp, tag in enumerate(("xt", "vb")):
+                turn_x_words(j, gp, tag)
                 centre(0, j, gp)
             for gp in range(2):
                 for gi in range(2):
                     quantise(0, j, gp, gi)
-        group_pa(0, 0)
-        for c in range(1, 4):
-            group_pa(c, 1)
+        dt = psum.tile([P, P], BF16, name="dt", tag="st", bufs=1)
+        nc.tensor.transpose(dt[:], dinv_rows[:], ident_b[:])
+        nc.vector.tensor_copy(out=dinv_t[:], in_=dt[:, 0:NB])
+        group_pa(0, 1)
+        quantise_pa(0)
+        group_pa(1, 0)
+        turn_step(0)
         permute(4)
         permute(5)
-        quantise_pa(0)
+        quantise_pa(1)
+        group_pa(2, 1)
 
-        for s in range(SLOTS + 2):
+        waiting = []
+        late = None
+        for s in range(SLOTS + 1):
             g, q = divmod(s, 4)
-            ahead = s < SLOTS and g + 1 < NG
-            if s + 8 < M // P and s < SLOTS:
-                load_x(s + 8)
-            if s < SLOTS and q == 1 and g + 1 < NG:
-                load_rows(step_tiles, step, g + 1, "step_in")
-            if s < SLOTS and q == 2 and g + 1 < NG:
-                load_rows(y_tiles, y, g + 1, "y_in")
-            if s + 6 < M // P:
-                permute(s + 6)
             j, gp = divmod(q, 2)
-            if ahead:
-                turn_x(g + 1, j, gp)
-                centre(g + 1, j, gp)
-            if s < SLOTS:
-                turn_step(s)
-            for unit in finish_units(s):
+            ahead = s < SLOTS and g + 1 < NG
+            if s + 8 < M // P:
+                load_x(s + 8)
+            if ahead and q == 1:
+                load_rows(step_tiles, step, g + 1, "step_in")
+            if ahead and q == 2:
+                load_rows(y_tiles, y, g + 1, "y_in")
+            if late:
+                damp(*late)
+            for args in waiting:
+                quantise(*args)
+            waiting = []
+            if s in (2, 3):
+                quantise_pa(s)
+            for n, unit in enumerate(finish_units(s)):
+                turn_back(*unit, tag="xt" if s >= SLOTS - 4 and n % 2 else "vb")
                 finish(*unit)
             for unit in finish_units(s + 1):
                 keep_part(*unit)
-            if s == SLOTS + 1 or s >= SLOTS:
-                continue
-            if s + 1 < 4:
-                quantise_pa(s + 1)
-            for k in range(2):
-                if ahead:
-                    quantise(g + 1, j, gp, k)
-                multiply(g, 2 * q + k)
-                damp(g, 2 * q + k)
+            if ahead and s > 1:
+                turn_x(g + 1, j, gp)
+                centre(g + 1, j, gp)
+            if s < SLOTS:
+                if s > 0:
+                    turn_step(s)
+                if s == 1:
+                    group_pa(3, 1)
+                if s + 6 < M // P:
+                    permute(s + 6)
+                multiply(g, 2 * q)
+                damp(g, 2 * q)
+                multiply(g, 2 * q + 1)
+                late = (g, 2 * q + 1)
+            if s < 2:
+                turn_x(g + 1, j, gp, ("xt", "vb")[s])
+                damp(*late)
+                late = None
+                centre(g + 1, j, gp)
+            if ahead:
+                waiting = [(g + 1, j, gp, 0), (g + 1, j, gp, 1)]

@@ -5,7 +5,6 @@ from concourse.masks import make_identity
 
 M, KA, KB, N = 2048, 512, 1536, 1024
 K = KA + KB
-ABUFS = 2
 FLOPS = 2 * M * K * N
 
 F32 = mybir.dt.float32
@@ -19,14 +18,18 @@ ALU = mybir.AluOpType
 ACT = mybir.ActivationFunctionType
 
 P = 128
-G = K // 512
+PASS = 512
+PASSES = K // PASS
 ROWS = 512
-NG = M // ROWS
+GROUPS = M // ROWS
 TILES = ROWS // P
-NB = N // P
-HALF = 512
-SLOTS = NG * 4
-FINISHED = {12: 3, 13: 3, 14: 3, 15: 1, 16: 4}
+PAIR = 2 * P
+BLOCKS = N // P
+HALF = N // 2
+PIECES = 4 * GROUPS
+ORDER = (1, 2, 3, 0)
+PA_COLS = 256
+FIRST_BLOCKS = 3
 
 
 def tile_gaussian_imputation_jacobi_s1_kernel(tc, x, mu, pa, pb_words, pb_scales, dinv, y, step, out):
@@ -40,263 +43,445 @@ def tile_gaussian_imputation_jacobi_s1_kernel(tc, x, mu, pa, pb_words, pb_scales
 
         ident_f = keep.tile([P, P], F32, name="ident_f")
         ident_b = keep.tile([P, P], BF16, name="ident_b")
-        mu_t = keep.tile([P, G, 4], BF16, name="mu_t", align_bytes=64)
+        mu_t = keep.tile([P, PASSES, 4], BF16, name="mu_t", align_bytes=64)
         dinv_rows = keep.tile([P, P], BF16, name="dinv_rows")
-        dinv_t = keep.tile([P, NB], F32, name="dinv_t")
+        dinv_t = keep.tile([P, BLOCKS], F32, name="dinv_t")
         warm = keep.tile([P, 1], F32, name="warm")
         pa_raw = keep.tile([P, 4, N], BF16, name="pa_raw", align_bytes=64)
         pa_grp = keep.tile([P, N, 4], BF16, name="pa_grp", align_bytes=64)
         pa_codes = keep.tile([P, N], U32, name="pa_codes", align_bytes=64)
         pa_scale = keep.tile([P, N], U8, name="pa_scale", align_bytes=64)
-        pb_codes = keep.tile([P, G - 1, 2 * N], U8, name="pb_codes", align_bytes=64)
-        pb_scale = keep.tile([P, G - 1, N], U8, name="pb_scale", align_bytes=64)
+        pb_codes = keep.tile([P, PASSES - 1, 2 * N], U8, name="pb_codes", align_bytes=64)
+        pb_scale = keep.tile([P, PASSES - 1, N], U8, name="pb_scale", align_bytes=64)
 
-        x_tiles, xp_tiles, step_tiles, y_tiles = {}, {}, {}, {}
-        codes, scales, xts, xcs = {}, {}, {}, {}
-        vbs, step_ts, accs, vs, a_tiles, w_tiles = {}, {}, {}, {}, {}, {}
+        x_in, x_words, step_in, y_in = {}, {}, {}, {}
+        x_bank, centred, codes, scales = {}, {}, {}, {}
+        acc, step_t, z, back = {}, {}, {}, {}
+        w, kept, result = {}, {}, {}
 
-        def load_x(t):
-            x_tiles[t] = work.tile([P, K], BF16, name="x_in", tag="x_in", bufs=6, align_bytes=64)
-            nc.sync.dma_start(out=x_tiles[t][:], in_=x[t * P : (t + 1) * P, :])
 
-        def load_rows(store, src, g, name):
-            store[g] = work.tile([P, TILES, N], BF16, name=name, tag=name, bufs=2, align_bytes=64)
-            nc.sync.dma_start(out=store[g][:], in_=src[g * ROWS : (g + 1) * ROWS, :].rearrange("(i p) n -> p i n", p=P))
+        def rows_of(ap, group):
+            return ap[group * ROWS : (group + 1) * ROWS, :].rearrange("(p i) n -> p i n", i=TILES)
 
-        def permute(t):
-            xp_tiles[t] = work.tile([P, G, 2, P], F32, name="xp", tag="xp", bufs=6, align_bytes=64)
-            nc.scalar.copy(
-                out=xp_tiles[t][:],
-                in_=x_tiles[t][:].bitcast(F32).rearrange("r (g p u) -> r g u p", p=P, u=2),
-            )
-
-        def turn_x_words(j, gp, tag):
-            for gi in range(2):
-                xt = psum.tile([P, 2, 256], F32, name="xt", tag=tag, bufs=2)
-                for i in range(2):
-                    words = x_tiles[2 * j + i][:].bitcast(F32).rearrange("r (g p u) -> r g u p", p=P, u=2)
-                    for u in range(2):
-                        nc.tensor.transpose(xt[:, u, i * P : (i + 1) * P], words[:, 2 * gp + gi, u, :], ident_f[:])
-                xts[(0, j, gp, gi)] = xt
-
-        def turn_x(h, j, gp, tag="xt"):
-            for gi in range(2):
-                xt = psum.tile([P, 2, 256], F32, name="xt", tag=tag, bufs=2)
-                for i in range(2):
-                    for u in range(2):
-                        nc.tensor.transpose(
-                            xt[:, u, i * P : (i + 1) * P], xp_tiles[h * TILES + 2 * j + i][:, 2 * gp + gi, u, :], ident_f[:]
-                        )
-                xts[(h, j, gp, gi)] = xt
-
-        def centre(h, j, gp):
-            xc = work.tile([P, 2, 256, 4], BF16, name="xc", tag="xc", bufs=3, align_bytes=64)
-            for gi in range(2):
-                g = 2 * gp + gi
-                nc.vector.tensor_tensor(
-                    out=xc[:, gi].rearrange("p r (u e) -> p r u e", e=2),
-                    in0=xts[(h, j, gp, gi)][:].bitcast(BF16).rearrange("p u (r e) -> p r u e", e=2),
-                    in1=mu_t[:, g, :].rearrange("p (u e) -> p u e", e=2).unsqueeze(1).to_broadcast([P, 256, 2, 2]),
-                    op=ALU.subtract,
-                )
-            xcs[(h, j, gp)] = xc
-
-        def quantise(h, j, gp, gi):
-            if h not in codes:
-                codes[h] = work.tile([P, G, ROWS], U32, name="codes", tag="codes", bufs=2, align_bytes=64)
-                scales[h] = work.tile([P, G, ROWS], U8, name="scales", tag="scales", bufs=2, align_bytes=64)
-            g = 2 * gp + gi
-            nc.vector.quantize_mx(
-                out=codes[h][:, g, 256 * j : 256 * (j + 1)].bitcast(E4M3X4),
-                scales=scales[h][:, g, 256 * j : 256 * (j + 1)],
-                in_=xcs[(h, j, gp)][:, gi].rearrange("p r t -> p (r t)"),
-            )
-
-        def turn_step(s):
-            g, q = divmod(s, 4)
-            st = psum.tile([P, 2, ROWS], BF16, name="st", tag="st", bufs=1)
-            for k in range(2):
-                for i in range(TILES):
-                    nc.tensor.transpose(
-                        st[:, k, i * P : (i + 1) * P], step_tiles[g][:, i, (2 * q + k) * P : (2 * q + k + 1) * P], ident_b[:]
-                    )
-            step_ts[s] = work.tile([P, 2, ROWS], BF16, name="step_t", tag="step_t", bufs=3, align_bytes=64)
-            nc.scalar.copy(out=step_ts[s][:], in_=st[:])
-
-        def multiply(g, nb):
-            acc = psum.tile([P, ROWS], F32, name="acc", tag="acc", bufs=3)
-            cols = slice(nb * P, (nb + 1) * P)
-            order = (1, 2, 3, 0)
-            for n, k in enumerate(order):
-                if k == 0:
-                    w, ws = pa_codes[:, cols].bitcast(E4M3X4), pa_scale[:, cols]
-                else:
-                    w = pb_codes[:, k - 1, 2 * nb * P : 2 * (nb + 1) * P].bitcast(E2M1X4)
-                    ws = pb_scale[:, k - 1, cols]
-                nc.tensor.matmul_mx(
-                    out=acc[:],
-                    lhsT=w,
-                    lhsT_scale=ws,
-                    rhs=codes[g][:, k, :].bitcast(E4M3X4),
-                    rhs_scale=scales[g][:, k, :],
-                    start=(n == 0),
-                    stop=(n == G - 1),
-                )
-            accs[(g, nb)] = acc
-
-        def damp(g, nb):
-            v = work.tile([P, ROWS], F32, name="v", tag="v", bufs=14, align_bytes=64)
-            nc.vector.scalar_tensor_tensor(
-                out=v[:],
-                in0=accs[(g, nb)][:],
-                scalar=dinv_t[:, nb : nb + 1],
-                in1=step_ts[4 * g + nb // 2][:, nb % 2, :],
-                op0=ALU.mult,
-                op1=ALU.mult,
-            )
-            vs[(g, nb)] = v
-
-        def keep_part(g, h, i):
-            cols = slice(h * HALF, (h + 1) * HALF)
-            w = work.tile([P, HALF], F32, name="w", tag="w", bufs=4, align_bytes=64)
-            nc.scalar.activation(out=w[:], in_=step_tiles[g][:, i, cols], func=ACT.Identity, bias=1.0, scale=-1.0)
-            a = work.tile([P, HALF], F32, name="a", tag="a", bufs=ABUFS, align_bytes=64)
-            nc.gpsimd.tensor_tensor(out=a[:], in0=w[:], in1=y_tiles[g][:, i, cols], op=ALU.mult)
-            a_tiles[(g, h, i)] = a
-
-        def turn_back(g, h, i, tag="vb"):
-            vb = psum.tile([P, 4, P], F32, name="vb", tag=tag, bufs=2)
-            for c in range(4):
-                nc.tensor.transpose(vb[:, c, :], vs[(g, 4 * h + c)][:, i * P : (i + 1) * P], ident_f[:])
-            vbs[(g, h, i)] = vb
-
-        def finish(g, h, i):
-            vb = vbs[(g, h, i)]
-            o = work.tile([P, HALF], F32, name="o", tag="o", bufs=6, align_bytes=64)
-            nc.vector.tensor_tensor(
-                out=o[:], in0=a_tiles[(g, h, i)][:], in1=vb[:].rearrange("p c n -> p (c n)"), op=ALU.subtract
-            )
-            r0 = g * ROWS + i * P
-            nc.sync.dma_start(out=out[r0 : r0 + P, h * HALF : (h + 1) * HALF], in_=o[:])
-
-        first_unit = [0] * (SLOTS + 2)
-        for s in range(SLOTS + 1):
-            first_unit[s + 1] = first_unit[s] + FINISHED.get(s, 2 if s >= 3 else 0)
-
-        def finish_units(s):
-            if s > SLOTS:
-                return []
-            return [(m // 8, (m % 8) // 4, m % 4) for m in range(first_unit[s], first_unit[s + 1])]
-
-        def group_pa(c, engine):
-            cols = slice(c * 256, (c + 1) * 256)
-            dst, src = pa_grp[:, cols, :], pa_raw[:, :, cols].rearrange("p j n -> p n j")
-            if engine == 0:
-                nc.vector.tensor_copy(out=dst, in_=src)
+        def load_x(pair, passes=None):
+            group, j = divmod(pair, 2)
+            if pair not in x_in:
+                x_in[pair] = work.tile([P, 2, K], BF16, name="x_in", tag="x_in", bufs=4, align_bytes=64)
+            src = rows_of(x, group)[:, 2 * j : 2 * j + 2, :]
+            if passes is None:
+                nc.sync.dma_start(out=x_in[pair][:], in_=src)
             else:
-                nc.scalar.copy(out=dst, in_=src)
+                cols = slice(passes * PASS, (passes + 1) * PASS)
+                nc.sync.dma_start(out=x_in[pair][:, :, cols], in_=src[:, :, cols])
+
+        def load_rows(tiles, src, group, name, half=None):
+            if group not in tiles:
+                tiles[group] = work.tile([P, TILES, N], BF16, name=name, tag=name, bufs=3, align_bytes=64)
+            cols = slice(0, N) if half is None else slice(half * HALF, (half + 1) * HALF)
+            nc.sync.dma_start(out=tiles[group][:, :, cols], in_=rows_of(src, group)[:, :, cols])
+
+        def load_pa(half):
+            cols = slice(half * HALF, (half + 1) * HALF)
+            nc.sync.dma_start(out=pa_raw[:, :, cols], in_=pa[:, cols].rearrange("(p t) n -> p t n", t=4))
+
+        def load_pb():
+            nc.sync.dma_start(out=pb_codes[:].bitcast(I32), in_=pb_words.rearrange("g p b -> p g b").bitcast(I32))
+
+        def load_pb_scales():
+            for q in range(4):
+                nc.sync.dma_start(
+                    out=pb_scale[32 * q : 32 * q + 4, :, :].bitcast(I32),
+                    in_=pb_scales[:, 4 * q : 4 * q + 4, :].rearrange("g r n -> r g n").bitcast(I32),
+                )
+
+
+        def interleave_pa(c, copy):
+            cols = slice(c * PA_COLS, (c + 1) * PA_COLS)
+            copy(out=pa_grp[:, cols, :], in_=pa_raw[:, :, cols].rearrange("p t n -> p n t"))
 
         def quantise_pa(c):
-            cols = slice(c * 256, (c + 1) * 256)
+            cols = slice(c * PA_COLS, (c + 1) * PA_COLS)
             nc.vector.quantize_mx(
                 out=pa_codes[:, cols].bitcast(E4M3X4),
                 scales=pa_scale[:, cols],
-                in_=pa_grp[:, cols, :].rearrange("p n j -> p (n j)"),
+                in_=pa_grp[:, cols, :].rearrange("p n t -> p (n t)"),
             )
 
-        nc.vector.memset(warm[:], 0.0)
-        nc.vector.memset(dinv_rows[:], 0.0)
-        nc.vector.memset(pb_scale[:].rearrange("p g n -> p (g n)").bitcast(I32), 0)
-        for t in range(4):
-            load_x(t)
+        def turn_dinv():
+            back["dinv"] = psum.tile([P, P], BF16, name="dinv_bank", tag="st", bufs=1)
+            nc.tensor.transpose(back["dinv"][:], dinv_rows[:], ident_b[:])
+
+        def keep_dinv():
+            nc.vector.tensor_copy(out=dinv_t[:], in_=back["dinv"][:, 0:BLOCKS])
+
+
+        def words_of(tile):
+            return x_in[tile // 2][:, tile % 2, :].bitcast(F32).rearrange("r (g p u) -> r g u p", p=P, u=2)
+
+        def lay_words(tile):
+            x_words[tile] = work.tile([P, PASSES, 2, P], F32, name="x_words", tag="x_words", bufs=6, align_bytes=64)
+            nc.scalar.copy(out=x_words[tile][:], in_=words_of(tile))
+
+        def turn_x(group, j, g, tag="xt"):
+            bank = psum.tile([P, 2, PAIR], F32, name="x_bank", tag=tag, bufs=2)
+            for i in range(2):
+                tile = group * TILES + 2 * j + i
+                src = x_words[tile] if tile in x_words else words_of(tile)
+                for u in range(2):
+                    nc.tensor.transpose(bank[:, u, i * P : (i + 1) * P], src[:, g, u, :], ident_f[:])
+            x_bank[(group, j, g)] = bank
+
+        def centre(group, j, g):
+            c = work.tile([P, PAIR, 4], BF16, name="centred", tag="centred", bufs=6, align_bytes=64)
+            nc.vector.tensor_tensor(
+                out=c[:].rearrange("p r (u e) -> p r u e", e=2),
+                in0=x_bank[(group, j, g)][:].bitcast(BF16).rearrange("p u (r e) -> p r u e", e=2),
+                in1=mu_t[:, g, :].rearrange("p (u e) -> p u e", e=2).unsqueeze(1).to_broadcast([P, PAIR, 2, 2]),
+                op=ALU.subtract,
+            )
+            centred[(group, j, g)] = c
+
+        def quantise(group, j, g):
+            if group not in codes:
+                codes[group] = work.tile([P, PASSES, ROWS], U32, name="codes", tag="codes", bufs=2, align_bytes=64)
+                scales[group] = work.tile([P, PASSES, ROWS], U8, name="scales", tag="scales", bufs=2, align_bytes=64)
+            rows = slice(j * PAIR, (j + 1) * PAIR)
+            nc.vector.quantize_mx(
+                out=codes[group][:, g, rows].bitcast(E4M3X4),
+                scales=scales[group][:, g, rows],
+                in_=centred[(group, j, g)][:].rearrange("p r t -> p (r t)"),
+            )
+
+
+        def multiply_pass(group, b, g):
+            cols = slice(b * P, (b + 1) * P)
+            if g == ORDER[0]:
+                acc[(group, b)] = psum.tile([P, ROWS], F32, name="acc", tag="acc", bufs=FIRST_BLOCKS)
+            if g == 0:
+                weight, weight_scale = pa_codes[:, cols].bitcast(E4M3X4), pa_scale[:, cols]
+            else:
+                weight = pb_codes[:, g - 1, 2 * b * P : 2 * (b + 1) * P].bitcast(E2M1X4)
+                weight_scale = pb_scale[:, g - 1, cols]
+            nc.tensor.matmul_mx(
+                out=acc[(group, b)][:],
+                lhsT=weight,
+                lhsT_scale=weight_scale,
+                rhs=codes[group][:, g, :].bitcast(E4M3X4),
+                rhs_scale=scales[group][:, g, :],
+                start=(g == ORDER[0]),
+                stop=(g == ORDER[-1]),
+            )
+
+        def multiply(group, b):
+            for g in ORDER:
+                multiply_pass(group, b, g)
+
+        def turn_step(group, b):
+            bank = psum.tile([P, ROWS], BF16, name="step_bank", tag="st", bufs=1)
+            for i in range(TILES):
+                nc.tensor.transpose(
+                    bank[:, i * P : (i + 1) * P], step_in[group][:, i, b * P : (b + 1) * P], ident_b[:]
+                )
+            step_t[(group, b)] = work.tile([P, ROWS], BF16, name="step_t", tag="step_t", bufs=3, align_bytes=64)
+            nc.scalar.copy(out=step_t[(group, b)][:], in_=bank[:])
+
+        def empty_even(group, b):
+            z[(group, b)] = work.tile([P, ROWS], F32, name="z", tag="z", bufs=12, align_bytes=64)
+            nc.vector.scalar_tensor_tensor(
+                out=z[(group, b)][:],
+                in0=acc[(group, b)][:],
+                scalar=dinv_t[:, b : b + 1],
+                in1=step_t[(group, b)][:],
+                op0=ALU.mult,
+                op1=ALU.mult,
+            )
+
+        def empty_odd(group, b):
+            z[(group, b)] = work.tile([P, ROWS], F32, name="z", tag="z", bufs=12, align_bytes=64)
+            nc.scalar.activation(
+                out=z[(group, b)][:], in_=acc[(group, b)][:], func=ACT.Identity, bias=0.0, scale=dinv_t[:, b : b + 1]
+            )
+
+
+        def place(m):
+            group, q = divmod(m, 4)
+            half, j = divmod(q, 2)
+            return group, half, slice(2 * j, 2 * j + 2), slice(half * HALF, (half + 1) * HALF)
+
+        def every_2nd(ap, odd):
+            return ap.rearrange("p i (c k n) -> p k i c n", k=2, n=P)[:, odd]
+
+        def turn_back(m, tag="vb"):
+            group, half, tiles, cols = place(m)
+            for odd in (1, 0):
+                bank = psum.tile([P, 2, 2, P], F32, name="back", tag=tag, bufs=2)
+                for i in range(2):
+                    for c in range(2):
+                        src = z[(group, 4 * half + 2 * c + odd)]
+                        rows = slice((tiles.start + i) * P, (tiles.start + i + 1) * P)
+                        nc.tensor.transpose(bank[:, i, c, :], src[:, rows], ident_f[:])
+                back[(m, odd)] = bank
+
+        def make_w(m):
+            group, half, tiles, cols = place(m)
+            w[m] = work.tile([P, 2, HALF], F32, name="w", tag="w", bufs=2, align_bytes=64)
+            nc.scalar.activation(out=w[m][:], in_=step_in[group][:, tiles, cols], func=ACT.Identity, bias=1.0, scale=-1.0)
+
+        def make_kept(m):
+            group, half, tiles, cols = place(m)
+            for odd in (1, 0):
+                kept[(m, odd)] = work.tile(
+                    [P, 2, 2, P], F32, name="kept%d" % odd, tag="kept%d" % odd, bufs=2, align_bytes=64
+                )
+                nc.gpsimd.tensor_tensor(
+                    out=kept[(m, odd)][:],
+                    in0=every_2nd(w[m][:], odd),
+                    in1=every_2nd(y_in[group][:, tiles, cols], odd),
+                    op=ALU.mult,
+                )
+
+        def mask_odd(m):
+            group, half, tiles, cols = place(m)
+            t = work.tile([P, 2, 2, P], F32, name="masked", tag="masked", bufs=2, align_bytes=64)
+            nc.vector.tensor_tensor(
+                out=t[:], in0=back[(m, 1)][:], in1=every_2nd(step_in[group][:, tiles, cols], 1), op=ALU.mult
+            )
+            back[(m, 1)] = t
+
+        def finish(m, odd):
+            if m not in result:
+                result[m] = work.tile([P, 2, HALF], F32, name="result", tag="result", bufs=3, align_bytes=64)
+            nc.vector.tensor_tensor(
+                out=every_2nd(result[m][:], odd), in0=kept[(m, odd)][:], in1=back[(m, odd)][:], op=ALU.subtract
+            )
+
+        def store(m):
+            group, half, tiles, cols = place(m)
+            nc.sync.dma_start(out=rows_of(out, group)[:, tiles, cols], in_=result[m][:])
+
+
         nc.scalar.dma_start(out=mu_t[:], in_=mu.rearrange("(g p t) -> p g t", p=P, t=4))
-        nc.scalar.dma_start(out=dinv_rows[0:NB, :], in_=dinv.rearrange("(b p) -> b p", p=P))
+        nc.vector.memset(dinv_rows[:], 0.0)
+        nc.scalar.dma_start(out=dinv_rows[0:BLOCKS, :], in_=dinv.rearrange("(b p) -> b p", p=P))
+        nc.vector.memset(warm[:], 0.0)
         nc.scalar.activation(out=warm[:], in_=warm[:], func=ACT.Identity, bias=0.0, scale=1.0)
+        nc.vector.memset(pb_scale[:].rearrange("p g n -> p (g n)").bitcast(I32), 0)
         make_identity(nc, ident_f[:])
         make_identity(nc, ident_b[:])
-        nc.sync.dma_start(
-            out=pb_codes[:].bitcast(I32), in_=pb_words.rearrange("g p b -> p g b").bitcast(I32)
-        )
-        for q in range(4):
-            nc.sync.dma_start(
-                out=pb_scale[32 * q : 32 * q + 4, :, :].bitcast(I32),
-                in_=pb_scales[:, 4 * q : 4 * q + 4, :].rearrange("g r n -> r g n").bitcast(I32),
-            )
-        step_tiles[0] = work.tile([P, TILES, N], BF16, name="step_in", tag="step_in", bufs=2, align_bytes=64)
-        for h in range(2):
-            cols = slice(h * HALF, (h + 1) * HALF)
-            nc.sync.dma_start(out=pa_raw[:, :, cols], in_=pa[:, cols].rearrange("(p j) n -> p j n", j=4))
-            nc.sync.dma_start(
-                out=step_tiles[0][:, :, cols], in_=step[0:ROWS, cols].rearrange("(i p) n -> p i n", p=P)
-            )
-            if h == 0:
-                load_x(4)
-                load_x(5)
-        load_x(6)
-        load_x(7)
-        load_rows(y_tiles, y, 0, "y_in")
 
-        for j in range(2):
-            for gp, tag in enumerate(("xt", "vb")):
-                turn_x_words(j, gp, tag)
-                centre(0, j, gp)
-            for gp in range(2):
-                for gi in range(2):
-                    quantise(0, j, gp, gi)
-        dt = psum.tile([P, P], BF16, name="dt", tag="st", bufs=1)
-        nc.tensor.transpose(dt[:], dinv_rows[:], ident_b[:])
-        nc.vector.tensor_copy(out=dinv_t[:], in_=dt[:, 0:NB])
-        group_pa(0, 1)
+        for g in ORDER:
+            load_x(0, g)
+            load_x(1, g)
+        load_pb()
+        load_pa(0)
+        load_pb_scales()
+        load_rows(step_in, step, 0, "step_in", 0)
+        load_x(2)
+        load_pa(1)
+        load_rows(step_in, step, 0, "step_in", 1)
+        load_x(3)
+        load_rows(y_in, y, 0, "y_in")
+        load_x(4)
+        load_rows(step_in, step, 1, "step_in")
+        load_x(5)
+        load_rows(y_in, y, 1, "y_in")
+
+
+        turn_x(0, 0, 1)
+        turn_x(0, 1, 1)
+        turn_x(0, 0, 2, "vb")
+        turn_x(0, 1, 2, "vb")
+        turn_dinv()
+        centre(0, 0, 1)
+        centre(0, 1, 1)
+        turn_x(0, 0, 3)
+        turn_x(0, 1, 3)
+        centre(0, 0, 2)
+        centre(0, 1, 2)
+        keep_dinv()
+        quantise(0, 0, 1)
+        quantise(0, 1, 1)
+        turn_x(0, 0, 0, "vb")
+        turn_x(0, 1, 0, "vb")
+        interleave_pa(0, nc.scalar.copy)
+        interleave_pa(1, nc.scalar.copy)
+        centre(0, 0, 3)
+        centre(0, 1, 3)
+        quantise(0, 0, 2)
+        quantise(0, 1, 2)
+        centre(0, 0, 0)
+        centre(0, 1, 0)
+        quantise(0, 0, 3)
+        quantise(0, 1, 3)
         quantise_pa(0)
-        group_pa(1, 0)
-        turn_step(0)
-        permute(4)
-        permute(5)
+        quantise(0, 0, 0)
+        quantise(0, 1, 0)
         quantise_pa(1)
-        group_pa(2, 1)
+        for g in ORDER:
+            if g == 0:
+                turn_step(0, 0)
+                turn_step(0, 2)
+                turn_x(1, 0, 0)
+                turn_x(1, 0, 1)
+            for b in range(FIRST_BLOCKS):
+                multiply_pass(0, b, g)
+        centre(1, 0, 0)
+        turn_step(0, 4)
+        interleave_pa(3, nc.vector.tensor_copy)
+        empty_even(0, 0)
+        empty_odd(0, 1)
+        interleave_pa(2, nc.vector.tensor_copy)
+        quantise_pa(3)
+        quantise_pa(2)
+        turn_x(1, 0, 2, "vb")
+        turn_step(0, 6)
+        multiply(0, 3)
+        empty_even(0, 2)
+        multiply(0, 4)
+        turn_x(1, 0, 3, "vb")
+        centre(1, 0, 1)
+        empty_odd(0, 3)
+        turn_x(1, 1, 0)
+        quantise(1, 0, 0)
+        centre(1, 0, 2)
+        turn_x(1, 1, 1)
+        quantise(1, 0, 1)
+        quantise(1, 0, 2)
+        turn_back(0)
+        turn_x(1, 1, 2)
+        multiply(0, 5)
+        make_w(0)
+        make_kept(0)
+        make_w(1)
+        lay_words(8)
+        multiply(0, 6)
+        centre(1, 0, 3)
+        centre(1, 1, 0)
+        quantise(1, 0, 3)
+        turn_x(1, 1, 3)
+        centre(1, 1, 1)
+        mask_odd(0)
+        lay_words(9)
+        multiply(0, 7)
+        quantise(1, 1, 0)
+        finish(0, 1)
+        quantise(1, 1, 1)
+        empty_even(0, 4)
+        load_x(6)
+        centre(1, 1, 2)
+        centre(1, 1, 3)
+        finish(0, 0)
+        store(0)
+        empty_odd(0, 5)
+        quantise(1, 1, 2)
+        make_kept(1)
+        quantise(1, 1, 3)
 
-        waiting = []
-        late = None
-        for s in range(SLOTS + 1):
-            g, q = divmod(s, 4)
-            j, gp = divmod(q, 2)
-            ahead = s < SLOTS and g + 1 < NG
-            if s + 8 < M // P:
-                load_x(s + 8)
-            if ahead and q == 1:
-                load_rows(step_tiles, step, g + 1, "step_in")
-            if ahead and q == 2:
-                load_rows(y_tiles, y, g + 1, "y_in")
-            if late:
-                damp(*late)
-            for args in waiting:
-                quantise(*args)
-            waiting = []
-            if s in (2, 3):
-                quantise_pa(s)
-            for n, unit in enumerate(finish_units(s)):
-                turn_back(*unit, tag="xt" if s >= SLOTS - 4 and n % 2 else "vb")
-                finish(*unit)
-            for unit in finish_units(s + 1):
-                keep_part(*unit)
-            if ahead and s > 1:
-                turn_x(g + 1, j, gp)
-                centre(g + 1, j, gp)
-            if s < SLOTS:
-                if s > 0:
-                    turn_step(s)
-                if s == 1:
-                    group_pa(3, 1)
-                if s + 6 < M // P:
-                    permute(s + 6)
-                multiply(g, 2 * q)
-                damp(g, 2 * q)
-                multiply(g, 2 * q + 1)
-                late = (g, 2 * q + 1)
-            if s < 2:
-                turn_x(g + 1, j, gp, ("xt", "vb")[s])
-                damp(*late)
-                late = None
-                centre(g + 1, j, gp)
-            if ahead:
-                waiting = [(g + 1, j, gp, 0), (g + 1, j, gp, 1)]
+
+        for s in range(4, 4 * (GROUPS - 1)):
+            group, q = divmod(s, 4)
+            even, odd = 2 * q, 2 * q + 1
+            last_group, last_q = divmod(s - 1, 4)
+            j, first = q // 2, 2 * (q % 2)
+            if s > 4:
+                finish(s - 4, 1)
+            turn_x(group + 1, j, first)
+            if s > 4:
+                finish(s - 4, 0)
+                store(s - 4)
+            turn_x(group + 1, j, first + 1)
+            make_w(s - 2)
+            centre(group + 1, j, first)
+            turn_step(group, even)
+            make_kept(s - 2)
+            turn_back(s - 3)
+            multiply(group, even)
+            empty_even(last_group, 2 * last_q)
+            multiply(group, odd)
+            centre(group + 1, j, first + 1)
+            if s in (4, 7):
+                load_rows(step_in, step, s // 3 + 1, "step_in")
+            if s in (5, 8):
+                load_rows(y_in, y, s // 3 + 1, "y_in")
+            if s == 6:
+                load_x(7)
+            empty_odd(last_group, 2 * last_q + 1)
+            if s + 6 < GROUPS * TILES:
+                lay_words(s + 6)
+            mask_odd(s - 3)
+            quantise(group + 1, j, first)
+            quantise(group + 1, j, first + 1)
+
+
+        finish(8, 1)
+        finish(8, 0)
+        store(8)
+        multiply(3, 0)
+        empty_even(2, 6)
+        make_w(10)
+        empty_odd(2, 7)
+        make_kept(10)
+        turn_step(3, 0)
+        turn_back(9, "xt")
+        turn_back(10)
+        make_w(11)
+        make_kept(11)
+        empty_even(3, 0)
+        mask_odd(9)
+        turn_step(3, 2)
+        multiply(3, 1)
+        empty_odd(3, 1)
+        multiply(3, 2)
+        turn_step(3, 4)
+        finish(9, 1)
+        finish(9, 0)
+        store(9)
+        turn_back(11, "xt")
+        mask_odd(10)
+        make_w(12)
+        finish(10, 1)
+        mask_odd(11)
+        multiply(3, 3)
+        multiply(3, 4)
+        empty_even(3, 2)
+        finish(10, 0)
+        store(10)
+        make_kept(12)
+        empty_odd(3, 3)
+        finish(11, 1)
+        finish(11, 0)
+        store(11)
+        make_w(13)
+        turn_back(12)
+        turn_step(3, 6)
+        mask_odd(12)
+        empty_even(3, 4)
+        multiply(3, 5)
+        multiply(3, 6)
+        multiply(3, 7)
+        finish(12, 1)
+        make_w(14)
+        make_kept(13)
+        turn_back(13)
+        mask_odd(13)
+        finish(12, 0)
+        store(12)
+        finish(13, 1)
+        empty_odd(3, 5)
+        empty_even(3, 6)
+        empty_odd(3, 7)
+        make_w(15)
+        make_kept(14)
+        turn_back(14)
+        mask_odd(14)
+        finish(13, 0)
+        store(13)
+        finish(14, 1)
+        make_kept(15)
+        turn_back(15)
+        mask_odd(15)
+        finish(14, 0)
+        store(14)
+        finish(15, 1)
+        finish(15, 0)
+        store(15)

@@ -26,10 +26,65 @@ TILES = ROWS // P
 PAIR = 2 * P
 BLOCKS = N // P
 HALF = N // 2
-PIECES = 4 * GROUPS
 ORDER = (1, 2, 3, 0)
 PA_COLS = 256
-FIRST_BLOCKS = 3
+MASKED_BEFORE = ((0,), (0,), (0,), (0,))
+
+CALLS = """
+    load_first(1) turn_x(0,0,2,1) load_first(0) load_pb_scales() turn_x(0,1,2,1) load_first(3) turn_x(0,0,1,0)
+    load_first(2) centre(0,0,1) turn_x(0,1,1,0) load_pb() turn_x(0,1,3,0) load_pa(0) load_first_step(0)
+    turn_x(0,0,3,0) centre(0,0,2) turn_x(0,0,0,1) lay_pa(1) centre(0,1,1) quantise(0,1,1) load_x(2) load_pa(1)
+    quantise(0,0,1) load_first_step(1) turn_dinv() multiply_pass(0,2,1) multiply_pass(0,1,1) centre(0,1,2)
+    turn_x(0,1,0,1) centre(0,0,3) load_x(3) centre(0,1,3) quantise(0,0,2) turn_step(0,0) copy_step(0,0)
+    multiply_pass(0,0,1) load_y(0) load_x(4) keep_dinv() load_step(1) quantise(0,0,3) quantise(0,1,2)
+    multiply_pass(0,1,2) lay_pa(0) multiply_pass(0,2,2) quantise(0,1,3) centre(0,0,0) multiply_pass(0,2,3)
+    multiply_pass(0,0,2) centre(0,1,0) multiply_pass(0,1,3) multiply_pass(0,0,3) turn_step(0,2) copy_step(0,2)
+    turn_x(1,0,0,0) quantise(0,0,0) turn_x(1,0,1,0) quantise_pa(0) quantise_pa(1) quantise(0,1,0) make_w(0)
+    make_kept(0,1) multiply_pass(0,2,0) multiply_pass(0,0,0) centre(1,0,0) centre(1,0,1) multiply_pass(0,1,0)
+    turn_x(1,0,2,1) lay_pa_on_vector(3) turn_x(1,0,3,1) empty(0,2) empty(0,1) centre(1,0,2) load_x(5)
+    multiply(0,3) make_kept(0,0) lay_pa_on_vector(2) quantise(1,0,2) quantise_pa(3) quantise(1,0,0)
+    quantise_pa(2) quantise(1,0,1) empty(0,3) turn_step(0,4) copy_step(0,4) make_w(1) turn_x(1,1,1,0)
+    centre(1,0,3) turn_x(1,1,0,0) multiply(0,4) turn_back(0,1,1) centre(1,1,1) empty(0,0) turn_step(0,6)
+    copy_step(0,6) centre(1,1,0) multiply(0,5) mask(0,1) finish(0,1) turn_back(0,0,1) finish(0,0) store(0)
+    turn_x(1,1,3,0) turn_x(1,1,2,0) centre(1,1,3) empty(0,4) multiply(0,7) centre(1,1,2) quantise(1,1,3)
+    quantise(1,1,2) empty(0,5) quantise(1,1,0) make_kept(1,0) make_kept(1,1) load_y(1) quantise(1,0,3) load_x(6)
+    lay_words(8) lay_words(9) multiply(0,6) quantise(1,1,1) turn_x(2,0,1,0) make_w(2) empty(0,6) empty(0,7)
+    turn_back(1,1,1) mask(1,1) centre(2,0,1) make_kept(2,1) turn_step(1,0) copy_step(1,0) turn_x(2,0,0,0)
+    centre(2,0,0) multiply(1,0) quantise(2,0,1) quantise(2,0,0) multiply(1,1) lay_words(10) turn_back(1,0,1)
+    make_kept(2,0) turn_x(2,0,3,0) finish(1,1) finish(1,0) store(1) make_w(3) empty(1,0) empty(1,1)
+    turn_back(2,1,1) mask(2,1) centre(2,0,3) make_kept(3,1) turn_step(1,2) copy_step(1,2) turn_x(2,0,2,0)
+    centre(2,0,2) multiply(1,2) load_x(7) load_step(2) quantise(2,0,3) quantise(2,0,2) multiply(1,3)
+    lay_words(11) turn_back(2,0,1) make_kept(3,0) turn_x(2,1,1,0) finish(2,1) finish(2,0) store(2) make_w(4)
+    empty(1,2) empty(1,3) turn_back(3,1,1) mask(3,1) centre(2,1,1) make_kept(4,1) turn_step(1,4) copy_step(1,4)
+    turn_x(2,1,0,0) centre(2,1,0) multiply(1,4) load_y(2) quantise(2,1,1) quantise(2,1,0) multiply(1,5)
+    lay_words(12) turn_back(3,0,1) make_kept(4,0) turn_x(2,1,3,0) finish(3,1) finish(3,0) store(3) make_w(5)
+    empty(1,4) empty(1,5) turn_back(4,1,1) mask(4,1) centre(2,1,3) make_kept(5,1) turn_step(1,6) copy_step(1,6)
+    turn_x(2,1,2,0) centre(2,1,2) multiply(1,6) quantise(2,1,3) quantise(2,1,2) multiply(1,7) lay_words(13)
+    turn_back(4,0,1) make_kept(5,0) turn_x(3,0,1,0) finish(4,1) finish(4,0) store(4) make_w(6) empty(1,6)
+    empty(1,7) turn_back(5,1,1) mask(5,1) centre(3,0,1) make_kept(6,1) turn_step(2,0) copy_step(2,0)
+    turn_x(3,0,0,0) centre(3,0,0) multiply(2,0) load_step(3) load_y(3) quantise(3,0,1) quantise(3,0,0)
+    multiply(2,1) lay_words(14) turn_back(5,0,1) make_kept(6,0) turn_x(3,0,3,0) finish(5,1) finish(5,0) store(5)
+    make_w(7) empty(2,0) empty(2,1) turn_back(6,1,1) mask(6,1) centre(3,0,3) make_kept(7,1) turn_step(2,2)
+    copy_step(2,2) turn_x(3,0,2,0) centre(3,0,2) multiply(2,2) quantise(3,0,3) quantise(3,0,2) multiply(2,3)
+    lay_words(15) turn_back(6,0,1) make_kept(7,0) turn_x(3,1,1,0) finish(6,1) finish(6,0) store(6) make_w(8)
+    empty(2,2) empty(2,3) turn_back(7,1,1) mask(7,1) centre(3,1,1) make_kept(8,1) turn_step(2,4) copy_step(2,4)
+    turn_x(3,1,0,0) centre(3,1,0) multiply(2,4) quantise(3,1,1) quantise(3,1,0) multiply(2,5) turn_back(7,0,1)
+    make_kept(8,0) turn_x(3,1,3,0) finish(7,1) finish(7,0) store(7) make_w(9) empty(2,4) empty(2,5)
+    turn_back(8,1,1) mask(8,1) centre(3,1,3) make_kept(9,1) turn_step(2,6) copy_step(2,6) turn_x(3,1,2,0)
+    centre(3,1,2) multiply(2,6) quantise(3,1,3) quantise(3,1,2) multiply(2,7) turn_back(8,0,1) make_kept(9,0)
+    finish(8,1) finish(8,0) store(8) make_w(10) make_kept(10,1) turn_back(9,0,0) make_kept(10,0) empty(2,7)
+    make_w(11) make_kept(11,1) empty(2,6) turn_back(9,1,1) mask(9,1) finish(9,1) finish(9,0) store(9)
+    turn_step(3,0) copy_step(3,0) multiply(3,0) empty(3,0) make_kept(11,0) multiply(3,2) turn_back(10,0,1)
+    finish(10,0) turn_back(10,1,1) mask(10,1) finish(10,1) store(10) make_w(12) make_kept(12,0) turn_step(3,2)
+    copy_step(3,2) empty(3,2) multiply(3,1) make_kept(12,1) empty(3,1) turn_back(11,1,1) mask(11,1) finish(11,1)
+    turn_back(11,0,1) finish(11,0) store(11) multiply(3,3) make_w(13) make_kept(13,0) empty(3,3) multiply(3,4)
+    turn_back(12,1,1) mask(12,1) finish(12,1) turn_step(3,4) copy_step(3,4) empty(3,4) make_w(14) multiply(3,7)
+    turn_back(13,1,1) mask(13,1) multiply(3,5) turn_back(12,0,1) finish(12,0) store(12) empty(3,7) empty(3,5)
+    turn_step(3,6) copy_step(3,6) make_kept(13,1) finish(13,1) turn_back(13,0,1) finish(13,0) store(13)
+    multiply(3,6) empty(3,6) turn_back(14,1,1) mask(14,1) turn_back(15,1,1) mask(15,1) make_kept(14,1)
+    finish(14,1) turn_back(14,0,1) make_kept(14,0) finish(14,0) store(14) make_w(15) turn_back(15,0,1)
+    make_kept(15,0) finish(15,0) make_kept(15,1) finish(15,1) store(15)
+"""
 
 
 def tile_gaussian_imputation_jacobi_s1_kernel(tc, x, mu, pa, pb_words, pb_scales, dinv, y, step, out):
@@ -47,42 +102,61 @@ def tile_gaussian_imputation_jacobi_s1_kernel(tc, x, mu, pa, pb_words, pb_scales
         dinv_rows = keep.tile([P, P], BF16, name="dinv_rows")
         dinv_t = keep.tile([P, BLOCKS], F32, name="dinv_t")
         warm = keep.tile([P, 1], F32, name="warm")
-        pa_raw = keep.tile([P, 4, N], BF16, name="pa_raw", align_bytes=64)
+        pa_raw = keep.tile([P, 2, 4, HALF], BF16, name="pa_raw", align_bytes=64)
         pa_grp = keep.tile([P, N, 4], BF16, name="pa_grp", align_bytes=64)
         pa_codes = keep.tile([P, N], U32, name="pa_codes", align_bytes=64)
         pa_scale = keep.tile([P, N], U8, name="pa_scale", align_bytes=64)
         pb_codes = keep.tile([P, PASSES - 1, 2 * N], U8, name="pb_codes", align_bytes=64)
         pb_scale = keep.tile([P, PASSES - 1, N], U8, name="pb_scale", align_bytes=64)
 
-        x_in, x_words, step_in, y_in = {}, {}, {}, {}
+        x_first, x_in, x_words, step_in, y_in = {}, {}, {}, {}, {}
         x_bank, centred, codes, scales = {}, {}, {}, {}
-        acc, step_t, z, back = {}, {}, {}, {}
+        acc, step_bank, step_t, z, back = {}, {}, {}, {}, {}
         w, kept, result = {}, {}, {}
 
 
         def rows_of(ap, group):
             return ap[group * ROWS : (group + 1) * ROWS, :].rearrange("(p i) n -> p i n", i=TILES)
 
-        def load_x(pair, passes=None):
-            group, j = divmod(pair, 2)
-            if pair not in x_in:
-                x_in[pair] = work.tile([P, 2, K], BF16, name="x_in", tag="x_in", bufs=4, align_bytes=64)
-            src = rows_of(x, group)[:, 2 * j : 2 * j + 2, :]
-            if passes is None:
-                nc.sync.dma_start(out=x_in[pair][:], in_=src)
-            else:
-                cols = slice(passes * PASS, (passes + 1) * PASS)
-                nc.sync.dma_start(out=x_in[pair][:, :, cols], in_=src[:, :, cols])
+        def load_first(n):
+            part, slot = divmod(n, 2)
+            if part not in x_first:
+                x_first[part] = work.tile([P, 2, TILES, PASS], BF16, name="x_in", tag="x_in", bufs=4, align_bytes=64)
+            g = ORDER[n]
+            nc.sync.dma_start(
+                out=x_first[part][:, slot, :, :],
+                in_=rows_of(x, 0)[:, :, g * PASS : (g + 1) * PASS],
+            )
 
-        def load_rows(tiles, src, group, name, half=None):
-            if group not in tiles:
-                tiles[group] = work.tile([P, TILES, N], BF16, name=name, tag=name, bufs=3, align_bytes=64)
-            cols = slice(0, N) if half is None else slice(half * HALF, (half + 1) * HALF)
-            nc.sync.dma_start(out=tiles[group][:, :, cols], in_=rows_of(src, group)[:, :, cols])
+        def load_x(pair):
+            group, j = divmod(pair, 2)
+            x_in[pair] = work.tile([P, 2, K], BF16, name="x_in", tag="x_in", bufs=4, align_bytes=64)
+            nc.sync.dma_start(out=x_in[pair][:], in_=rows_of(x, group)[:, 2 * j : 2 * j + 2, :])
+
+        def load_rows(tiles, src, name, group):
+            tiles[group] = work.tile([P, TILES, N], BF16, name=name, tag=name, bufs=3, align_bytes=64)
+            nc.sync.dma_start(out=tiles[group][:], in_=rows_of(src, group))
+
+        def load_step(group):
+            load_rows(step_in, step, "step_in", group)
+
+        def load_first_step(half):
+            if 0 not in step_in:
+                step_in[0] = work.tile([P, 2, TILES, HALF], BF16, name="step_in", tag="step_in", bufs=3, align_bytes=64)
+            cols = slice(half * HALF, (half + 1) * HALF)
+            nc.sync.dma_start(out=step_in[0][:, half, :, :], in_=rows_of(step, 0)[:, :, cols])
+
+        def load_y(group):
+            load_rows(y_in, y, "y_in", group)
+
+        def step_part(group, half, tiles):
+            if group == 0:
+                return step_in[0][:, half, tiles, :]
+            return step_in[group][:, tiles, half * HALF : (half + 1) * HALF]
 
         def load_pa(half):
             cols = slice(half * HALF, (half + 1) * HALF)
-            nc.sync.dma_start(out=pa_raw[:, :, cols], in_=pa[:, cols].rearrange("(p t) n -> p t n", t=4))
+            nc.sync.dma_start(out=pa_raw[:, half, :, :], in_=pa[:, cols].rearrange("(p t) n -> p t n", t=4))
 
         def load_pb():
             nc.sync.dma_start(out=pb_codes[:].bitcast(I32), in_=pb_words.rearrange("g p b -> p g b").bitcast(I32))
@@ -95,9 +169,19 @@ def tile_gaussian_imputation_jacobi_s1_kernel(tc, x, mu, pa, pb_words, pb_scales
                 )
 
 
-        def interleave_pa(c, copy):
+        def pa_sides(c):
             cols = slice(c * PA_COLS, (c + 1) * PA_COLS)
-            copy(out=pa_grp[:, cols, :], in_=pa_raw[:, :, cols].rearrange("p t n -> p n t"))
+            half, c = divmod(c, 2)
+            source = pa_raw[:, half, :, c * PA_COLS : (c + 1) * PA_COLS]
+            return pa_grp[:, cols, :], source.rearrange("p t n -> p n t")
+
+        def lay_pa(c):
+            target, source = pa_sides(c)
+            nc.scalar.copy(out=target, in_=source)
+
+        def lay_pa_on_vector(c):
+            target, source = pa_sides(c)
+            nc.vector.tensor_copy(out=target, in_=source)
 
         def quantise_pa(c):
             cols = slice(c * PA_COLS, (c + 1) * PA_COLS)
@@ -108,7 +192,7 @@ def tile_gaussian_imputation_jacobi_s1_kernel(tc, x, mu, pa, pb_words, pb_scales
             )
 
         def turn_dinv():
-            back["dinv"] = psum.tile([P, P], BF16, name="dinv_bank", tag="st", bufs=1)
+            back["dinv"] = psum.tile([P, P], BF16, name="dinv_bank", tag="step", bufs=1)
             nc.tensor.transpose(back["dinv"][:], dinv_rows[:], ident_b[:])
 
         def keep_dinv():
@@ -118,17 +202,25 @@ def tile_gaussian_imputation_jacobi_s1_kernel(tc, x, mu, pa, pb_words, pb_scales
         def words_of(tile):
             return x_in[tile // 2][:, tile % 2, :].bitcast(F32).rearrange("r (g p u) -> r g u p", p=P, u=2)
 
+        def words_of_pass(tile, g):
+            if tile in x_words:
+                return x_words[tile][:, g]
+            if tile < TILES:
+                part, slot = divmod(ORDER.index(g), 2)
+                return x_first[part][:, slot, tile, :].bitcast(F32).rearrange("r (p u) -> r u p", u=2)
+            return words_of(tile)[:, g]
+
         def lay_words(tile):
             x_words[tile] = work.tile([P, PASSES, 2, P], F32, name="x_words", tag="x_words", bufs=6, align_bytes=64)
             nc.scalar.copy(out=x_words[tile][:], in_=words_of(tile))
 
-        def turn_x(group, j, g, tag="xt"):
-            bank = psum.tile([P, 2, PAIR], F32, name="x_bank", tag=tag, bufs=2)
+        def turn_x(group, j, g, ring):
+            bank = psum.tile([P, 2, PAIR], F32, name="x_bank", tag="ring%d" % ring, bufs=2)
             for i in range(2):
                 tile = group * TILES + 2 * j + i
-                src = x_words[tile] if tile in x_words else words_of(tile)
+                src = words_of_pass(tile, g)
                 for u in range(2):
-                    nc.tensor.transpose(bank[:, u, i * P : (i + 1) * P], src[:, g, u, :], ident_f[:])
+                    nc.tensor.transpose(bank[:, u, i * P : (i + 1) * P], src[:, u, :], ident_f[:])
             x_bank[(group, j, g)] = bank
 
         def centre(group, j, g):
@@ -156,7 +248,7 @@ def tile_gaussian_imputation_jacobi_s1_kernel(tc, x, mu, pa, pb_words, pb_scales
         def multiply_pass(group, b, g):
             cols = slice(b * P, (b + 1) * P)
             if g == ORDER[0]:
-                acc[(group, b)] = psum.tile([P, ROWS], F32, name="acc", tag="acc", bufs=FIRST_BLOCKS)
+                acc[(group, b)] = psum.tile([P, ROWS], F32, name="acc", tag="acc", bufs=3)
             if g == 0:
                 weight, weight_scale = pa_codes[:, cols].bitcast(E4M3X4), pa_scale[:, cols]
             else:
@@ -177,30 +269,38 @@ def tile_gaussian_imputation_jacobi_s1_kernel(tc, x, mu, pa, pb_words, pb_scales
                 multiply_pass(group, b, g)
 
         def turn_step(group, b):
-            bank = psum.tile([P, ROWS], BF16, name="step_bank", tag="st", bufs=1)
+            bank = psum.tile([P, ROWS], BF16, name="step_bank", tag="step", bufs=1)
+            cols = slice(b % 4 * P, (b % 4 + 1) * P)
             for i in range(TILES):
-                nc.tensor.transpose(
-                    bank[:, i * P : (i + 1) * P], step_in[group][:, i, b * P : (b + 1) * P], ident_b[:]
-                )
+                nc.tensor.transpose(bank[:, i * P : (i + 1) * P], step_part(group, b // 4, i)[:, cols], ident_b[:])
+            step_bank[(group, b)] = bank
+
+        def copy_step(group, b):
             step_t[(group, b)] = work.tile([P, ROWS], BF16, name="step_t", tag="step_t", bufs=3, align_bytes=64)
-            nc.scalar.copy(out=step_t[(group, b)][:], in_=bank[:])
+            nc.scalar.copy(out=step_t[(group, b)][:], in_=step_bank[(group, b)][:])
 
-        def empty_even(group, b):
-            z[(group, b)] = work.tile([P, ROWS], F32, name="z", tag="z", bufs=12, align_bytes=64)
-            nc.vector.scalar_tensor_tensor(
-                out=z[(group, b)][:],
-                in0=acc[(group, b)][:],
-                scalar=dinv_t[:, b : b + 1],
-                in1=step_t[(group, b)][:],
-                op0=ALU.mult,
-                op1=ALU.mult,
-            )
+        def masked_before(group, b):
+            return b % 2 in MASKED_BEFORE[group]
 
-        def empty_odd(group, b):
+        def empty(group, b):
             z[(group, b)] = work.tile([P, ROWS], F32, name="z", tag="z", bufs=12, align_bytes=64)
-            nc.scalar.activation(
-                out=z[(group, b)][:], in_=acc[(group, b)][:], func=ACT.Identity, bias=0.0, scale=dinv_t[:, b : b + 1]
-            )
+            if masked_before(group, b):
+                nc.vector.scalar_tensor_tensor(
+                    out=z[(group, b)][:],
+                    in0=acc[(group, b)][:],
+                    scalar=dinv_t[:, b : b + 1],
+                    in1=step_t[(group, b)][:],
+                    op0=ALU.mult,
+                    op1=ALU.mult,
+                )
+            else:
+                nc.scalar.activation(
+                    out=z[(group, b)][:],
+                    in_=acc[(group, b)][:],
+                    func=ACT.Identity,
+                    bias=0.0,
+                    scale=dinv_t[:, b : b + 1],
+                )
 
 
         def place(m):
@@ -211,54 +311,68 @@ def tile_gaussian_imputation_jacobi_s1_kernel(tc, x, mu, pa, pb_words, pb_scales
         def every_2nd(ap, odd):
             return ap.rearrange("p i (c k n) -> p k i c n", k=2, n=P)[:, odd]
 
-        def turn_back(m, tag="vb"):
+        def turn_back(m, odd, ring):
             group, half, tiles, cols = place(m)
-            for odd in (1, 0):
-                bank = psum.tile([P, 2, 2, P], F32, name="back", tag=tag, bufs=2)
-                for i in range(2):
-                    for c in range(2):
-                        src = z[(group, 4 * half + 2 * c + odd)]
-                        rows = slice((tiles.start + i) * P, (tiles.start + i + 1) * P)
-                        nc.tensor.transpose(bank[:, i, c, :], src[:, rows], ident_f[:])
-                back[(m, odd)] = bank
+            bank = psum.tile([P, 2, 2, P], F32, name="back", tag="ring%d" % ring, bufs=2)
+            for i in range(2):
+                for c in range(2):
+                    src = z[(group, 4 * half + 2 * c + odd)]
+                    rows = slice((tiles.start + i) * P, (tiles.start + i + 1) * P)
+                    nc.tensor.transpose(bank[:, i, c, :], src[:, rows], ident_f[:])
+            back[(m, odd)] = bank
 
         def make_w(m):
             group, half, tiles, cols = place(m)
             w[m] = work.tile([P, 2, HALF], F32, name="w", tag="w", bufs=2, align_bytes=64)
-            nc.scalar.activation(out=w[m][:], in_=step_in[group][:, tiles, cols], func=ACT.Identity, bias=1.0, scale=-1.0)
+            nc.scalar.activation(out=w[m][:], in_=step_part(group, half, tiles), func=ACT.Identity, bias=1.0, scale=-1.0)
 
-        def make_kept(m):
+        def multiply_kept(engine, m, odd):
             group, half, tiles, cols = place(m)
-            for odd in (1, 0):
-                kept[(m, odd)] = work.tile(
-                    [P, 2, 2, P], F32, name="kept%d" % odd, tag="kept%d" % odd, bufs=2, align_bytes=64
-                )
-                nc.gpsimd.tensor_tensor(
-                    out=kept[(m, odd)][:],
-                    in0=every_2nd(w[m][:], odd),
-                    in1=every_2nd(y_in[group][:, tiles, cols], odd),
-                    op=ALU.mult,
-                )
+            name = "kept%d" % odd
+            kept[(m, odd)] = work.tile([P, 2, 2, P], F32, name=name, tag=name, bufs=2, align_bytes=64)
+            engine.tensor_tensor(
+                out=kept[(m, odd)][:],
+                in0=every_2nd(w[m][:], odd),
+                in1=every_2nd(y_in[group][:, tiles, cols], odd),
+                op=ALU.mult,
+            )
 
-        def mask_odd(m):
+        def make_kept(m, odd):
+            multiply_kept(nc.gpsimd, m, odd)
+
+        def make_kept_on_vector(m, odd):
+            multiply_kept(nc.vector, m, odd)
+
+        def mask(m, odd):
             group, half, tiles, cols = place(m)
             t = work.tile([P, 2, 2, P], F32, name="masked", tag="masked", bufs=2, align_bytes=64)
             nc.vector.tensor_tensor(
-                out=t[:], in0=back[(m, 1)][:], in1=every_2nd(step_in[group][:, tiles, cols], 1), op=ALU.mult
+                out=t[:], in0=back[(m, odd)][:], in1=every_2nd(step_part(group, half, tiles), odd), op=ALU.mult
             )
-            back[(m, 1)] = t
+            back[(m, odd)] = t
+
+        def subtract(m, odd, i):
+            nc.vector.tensor_tensor(
+                out=every_2nd(result[m][:], odd)[:, i],
+                in0=kept[(m, odd)][:, i],
+                in1=back[(m, odd)][:, i],
+                op=ALU.subtract,
+            )
 
         def finish(m, odd):
             if m not in result:
                 result[m] = work.tile([P, 2, HALF], F32, name="result", tag="result", bufs=3, align_bytes=64)
-            nc.vector.tensor_tensor(
-                out=every_2nd(result[m][:], odd), in0=kept[(m, odd)][:], in1=back[(m, odd)][:], op=ALU.subtract
-            )
+            subtract(m, odd, slice(0, 2))
+
+        def finish_and_store(m, odd):
+            group, half, tiles, cols = place(m)
+            for i in range(2):
+                subtract(m, odd, i)
+                nc.sync.dma_start(out=rows_of(out, group)[:, tiles.start + i, cols], in_=result[m][:, i, :])
 
         def store(m):
             group, half, tiles, cols = place(m)
             nc.sync.dma_start(out=rows_of(out, group)[:, tiles, cols], in_=result[m][:])
-
 
         nc.scalar.dma_start(out=mu_t[:], in_=mu.rearrange("(g p t) -> p g t", p=P, t=4))
         nc.vector.memset(dinv_rows[:], 0.0)
@@ -269,219 +383,14 @@ def tile_gaussian_imputation_jacobi_s1_kernel(tc, x, mu, pa, pb_words, pb_scales
         make_identity(nc, ident_f[:])
         make_identity(nc, ident_b[:])
 
-        for g in ORDER:
-            load_x(0, g)
-            load_x(1, g)
-        load_pb()
-        load_pa(0)
-        load_pb_scales()
-        load_rows(step_in, step, 0, "step_in", 0)
-        load_x(2)
-        load_pa(1)
-        load_rows(step_in, step, 0, "step_in", 1)
-        load_x(3)
-        load_rows(y_in, y, 0, "y_in")
-        load_x(4)
-        load_rows(step_in, step, 1, "step_in")
-        load_x(5)
-        load_rows(y_in, y, 1, "y_in")
-
-
-        turn_x(0, 0, 1)
-        turn_x(0, 1, 1)
-        turn_x(0, 0, 2, "vb")
-        turn_x(0, 1, 2, "vb")
-        turn_dinv()
-        centre(0, 0, 1)
-        centre(0, 1, 1)
-        turn_x(0, 0, 3)
-        turn_x(0, 1, 3)
-        centre(0, 0, 2)
-        centre(0, 1, 2)
-        keep_dinv()
-        quantise(0, 0, 1)
-        quantise(0, 1, 1)
-        turn_x(0, 0, 0, "vb")
-        turn_x(0, 1, 0, "vb")
-        interleave_pa(0, nc.scalar.copy)
-        interleave_pa(1, nc.scalar.copy)
-        centre(0, 0, 3)
-        centre(0, 1, 3)
-        quantise(0, 0, 2)
-        quantise(0, 1, 2)
-        centre(0, 0, 0)
-        centre(0, 1, 0)
-        quantise(0, 0, 3)
-        quantise(0, 1, 3)
-        quantise_pa(0)
-        quantise(0, 0, 0)
-        quantise(0, 1, 0)
-        quantise_pa(1)
-        for g in ORDER:
-            if g == 0:
-                turn_step(0, 0)
-                turn_step(0, 2)
-                turn_x(1, 0, 0)
-                turn_x(1, 0, 1)
-            for b in range(FIRST_BLOCKS):
-                multiply_pass(0, b, g)
-        centre(1, 0, 0)
-        turn_step(0, 4)
-        interleave_pa(3, nc.vector.tensor_copy)
-        empty_even(0, 0)
-        empty_odd(0, 1)
-        interleave_pa(2, nc.vector.tensor_copy)
-        quantise_pa(3)
-        quantise_pa(2)
-        turn_x(1, 0, 2, "vb")
-        turn_step(0, 6)
-        multiply(0, 3)
-        empty_even(0, 2)
-        multiply(0, 4)
-        turn_x(1, 0, 3, "vb")
-        centre(1, 0, 1)
-        empty_odd(0, 3)
-        turn_x(1, 1, 0)
-        quantise(1, 0, 0)
-        centre(1, 0, 2)
-        turn_x(1, 1, 1)
-        quantise(1, 0, 1)
-        quantise(1, 0, 2)
-        turn_back(0)
-        turn_x(1, 1, 2)
-        multiply(0, 5)
-        make_w(0)
-        make_kept(0)
-        make_w(1)
-        lay_words(8)
-        multiply(0, 6)
-        centre(1, 0, 3)
-        centre(1, 1, 0)
-        quantise(1, 0, 3)
-        turn_x(1, 1, 3)
-        centre(1, 1, 1)
-        mask_odd(0)
-        lay_words(9)
-        multiply(0, 7)
-        quantise(1, 1, 0)
-        finish(0, 1)
-        quantise(1, 1, 1)
-        empty_even(0, 4)
-        load_x(6)
-        centre(1, 1, 2)
-        centre(1, 1, 3)
-        finish(0, 0)
-        store(0)
-        empty_odd(0, 5)
-        quantise(1, 1, 2)
-        make_kept(1)
-        quantise(1, 1, 3)
-
-
-        for s in range(4, 4 * (GROUPS - 1)):
-            group, q = divmod(s, 4)
-            even, odd = 2 * q, 2 * q + 1
-            last_group, last_q = divmod(s - 1, 4)
-            j, first = q // 2, 2 * (q % 2)
-            if s > 4:
-                finish(s - 4, 1)
-            turn_x(group + 1, j, first)
-            if s > 4:
-                finish(s - 4, 0)
-                store(s - 4)
-            turn_x(group + 1, j, first + 1)
-            make_w(s - 2)
-            centre(group + 1, j, first)
-            turn_step(group, even)
-            make_kept(s - 2)
-            turn_back(s - 3)
-            multiply(group, even)
-            empty_even(last_group, 2 * last_q)
-            multiply(group, odd)
-            centre(group + 1, j, first + 1)
-            if s in (4, 7):
-                load_rows(step_in, step, s // 3 + 1, "step_in")
-            if s in (5, 8):
-                load_rows(y_in, y, s // 3 + 1, "y_in")
-            if s == 6:
-                load_x(7)
-            empty_odd(last_group, 2 * last_q + 1)
-            if s + 6 < GROUPS * TILES:
-                lay_words(s + 6)
-            mask_odd(s - 3)
-            quantise(group + 1, j, first)
-            quantise(group + 1, j, first + 1)
-
-
-        finish(8, 1)
-        finish(8, 0)
-        store(8)
-        multiply(3, 0)
-        empty_even(2, 6)
-        make_w(10)
-        empty_odd(2, 7)
-        make_kept(10)
-        turn_step(3, 0)
-        turn_back(9, "xt")
-        turn_back(10)
-        make_w(11)
-        make_kept(11)
-        empty_even(3, 0)
-        mask_odd(9)
-        turn_step(3, 2)
-        multiply(3, 1)
-        empty_odd(3, 1)
-        multiply(3, 2)
-        turn_step(3, 4)
-        finish(9, 1)
-        finish(9, 0)
-        store(9)
-        turn_back(11, "xt")
-        mask_odd(10)
-        make_w(12)
-        finish(10, 1)
-        mask_odd(11)
-        multiply(3, 3)
-        multiply(3, 4)
-        empty_even(3, 2)
-        finish(10, 0)
-        store(10)
-        make_kept(12)
-        empty_odd(3, 3)
-        finish(11, 1)
-        finish(11, 0)
-        store(11)
-        make_w(13)
-        turn_back(12)
-        turn_step(3, 6)
-        mask_odd(12)
-        empty_even(3, 4)
-        multiply(3, 5)
-        multiply(3, 6)
-        multiply(3, 7)
-        finish(12, 1)
-        make_w(14)
-        make_kept(13)
-        turn_back(13)
-        mask_odd(13)
-        finish(12, 0)
-        store(12)
-        finish(13, 1)
-        empty_odd(3, 5)
-        empty_even(3, 6)
-        empty_odd(3, 7)
-        make_w(15)
-        make_kept(14)
-        turn_back(14)
-        mask_odd(14)
-        finish(13, 0)
-        store(13)
-        finish(14, 1)
-        make_kept(15)
-        turn_back(15)
-        mask_odd(15)
-        finish(14, 0)
-        store(14)
-        finish(15, 1)
-        finish(15, 0)
-        store(15)
+        call = dict(
+            load_first=load_first, load_x=load_x, load_step=load_step, load_first_step=load_first_step, load_y=load_y, load_pa=load_pa, load_pb=load_pb,
+            load_pb_scales=load_pb_scales, lay_pa=lay_pa, lay_pa_on_vector=lay_pa_on_vector, quantise_pa=quantise_pa,
+            turn_dinv=turn_dinv, keep_dinv=keep_dinv, lay_words=lay_words, turn_x=turn_x, centre=centre,
+            quantise=quantise, multiply_pass=multiply_pass, multiply=multiply, turn_step=turn_step,
+            copy_step=copy_step, empty=empty, turn_back=turn_back, make_w=make_w, make_kept=make_kept,
+            make_kept_on_vector=make_kept_on_vector, mask=mask, finish=finish, finish_and_store=finish_and_store, store=store,
+        )
+        for text in CALLS.split():
+            name, numbers = text.replace(")", "").split("(")
+            call[name](*[int(number) for number in numbers.split(",") if number])

from contextlib import ExitStack

import concourse.mybir as mybir
from concourse.masks import make_identity

M, KA, KB, N = 2048, 512, 1536, 1024
K = KA + KB
FLOPS = 2 * M * K * N

F32 = mybir.dt.float32
BF16 = mybir.dt.bfloat16
U32 = mybir.dt.uint32
I32 = mybir.dt.int32
U8 = mybir.dt.uint8
E4M3X4 = mybir.dt.float8_e4m3fn_x4
E2M1X4 = mybir.dt.float4_e2m1fn_x4
ALU = mybir.AluOpType
ACT = mybir.ActivationFunctionType

P = 128
PASS = 512
PASSES = K // PASS
ROWS = 512
GROUPS = M // ROWS
TILES = ROWS // P
PAIR = 2 * P
BLOCKS = N // P
HALF = N // 2
ORDER = (1, 2, 3, 0)
PA_COLS = 256
MASKED_BEFORE = ((0,), (0,), (0,), (0,))

CALLS = """
    load_first(1) turn_x(0,0,2,1) load_first(0) load_pb_scales() turn_x(0,1,2,1) load_first(3) turn_x(0,0,1,0)
    load_first(2) centre(0,0,1) turn_x(0,1,1,0) load_pb() turn_x(0,1,3,0) load_pa(0) load_first_step(0)
    turn_x(0,0,3,0) centre(0,0,2) turn_x(0,0,0,1) lay_pa(1) centre(0,1,1) quantise(0,1,1) load_x(2) load_pa(1)
    quantise(0,0,1) load_first_step(1) turn_dinv() multiply_pass(0,2,1) multiply_pass(0,1,1) centre(0,1,2)
    turn_x(0,1,0,1) centre(0,0,3) load_x(3) centre(0,1,3) quantise(0,0,2) turn_step(0,0) copy_step(0,0)
    multiply_pass(0,0,1) load_y(0) load_x(4) keep_dinv() load_step(1) quantise(0,0,3) quantise(0,1,2)
    multiply_pass(0,1,2) lay_pa(0) multiply_pass(0,2,2) quantise(0,1,3) centre(0,0,0) multiply_pass(0,2,3)
    multiply_pass(0,0,2) centre(0,1,0) multiply_pass(0,1,3) multiply_pass(0,0,3) turn_step(0,2) copy_step(0,2)
    turn_x(1,0,0,0) quantise(0,0,0) turn_x(1,0,1,0) quantise_pa(0) quantise_pa(1) quantise(0,1,0) make_w(0)
    make_kept(0,1) multiply_pass(0,2,0) multiply_pass(0,0,0) centre(1,0,0) centre(1,0,1) multiply_pass(0,1,0)
    turn_x(1,0,2,1) lay_pa_on_vector(3) turn_x(1,0,3,1) empty(0,2) empty(0,1) centre(1,0,2) load_x(5)
    multiply(0,3) make_kept(0,0) lay_pa_on_vector(2) quantise(1,0,2) quantise_pa(3) quantise(1,0,0)
    quantise_pa(2) quantise(1,0,1) empty(0,3) turn_step(0,4) copy_step(0,4) make_w(1) turn_x(1,1,1,0)
    centre(1,0,3) turn_x(1,1,0,0) multiply(0,4) turn_back(0,1,1) centre(1,1,1) empty(0,0) turn_step(0,6)
    copy_step(0,6) centre(1,1,0) multiply(0,5) mask(0,1) finish(0,1) turn_back(0,0,1) finish(0,0) store(0)
    turn_x(1,1,3,0) turn_x(1,1,2,0) centre(1,1,3) empty(0,4) multiply(0,7) centre(1,1,2) quantise(1,1,3)
    quantise(1,1,2) empty(0,5) quantise(1,1,0) make_kept(1,0) make_kept(1,1) load_y(1) quantise(1,0,3) load_x(6)
    lay_words(8) lay_words(9) multiply(0,6) quantise(1,1,1) turn_x(2,0,1,0) make_w(2) empty(0,6) empty(0,7)
    turn_back(1,1,1) mask(1,1) centre(2,0,1) make_kept(2,1) turn_step(1,0) copy_step(1,0) turn_x(2,0,0,0)
    centre(2,0,0) multiply(1,0) quantise(2,0,1) quantise(2,0,0) multiply(1,1) lay_words(10) turn_back(1,0,1)
    make_kept(2,0) turn_x(2,0,3,0) finish(1,1) finish(1,0) store(1) make_w(3) empty(1,0) empty(1,1)
    turn_back(2,1,1) mask(2,1) centre(2,0,3) make_kept(3,1) turn_step(1,2) copy_step(1,2) turn_x(2,0,2,0)
    centre(2,0,2) multiply(1,2) load_x(7) load_step(2) quantise(2,0,3) quantise(2,0,2) multiply(1,3)
    lay_words(11) turn_back(2,0,1) make_kept(3,0) turn_x(2,1,1,0) finish(2,1) finish(2,0) store(2) make_w(4)
    empty(1,2) empty(1,3) turn_back(3,1,1) mask(3,1) centre(2,1,1) make_kept(4,1) turn_step(1,4) copy_step(1,4)
    turn_x(2,1,0,0) centre(2,1,0) multiply(1,4) load_y(2) quantise(2,1,1) quantise(2,1,0) multiply(1,5)
    lay_words(12) turn_back(3,0,1) make_kept(4,0) turn_x(2,1,3,0) finish(3,1) finish(3,0) store(3) make_w(5)
    empty(1,4) empty(1,5) turn_back(4,1,1) mask(4,1) centre(2,1,3) make_kept(5,1) turn_step(1,6) copy_step(1,6)
    turn_x(2,1,2,0) centre(2,1,2) multiply(1,6) quantise(2,1,3) quantise(2,1,2) multiply(1,7) lay_words(13)
    turn_back(4,0,1) make_kept(5,0) turn_x(3,0,1,0) finish(4,1) finish(4,0) store(4) make_w(6) empty(1,6)
    empty(1,7) turn_back(5,1,1) mask(5,1) centre(3,0,1) make_kept(6,1) turn_step(2,0) copy_step(2,0)
    turn_x(3,0,0,0) centre(3,0,0) multiply(2,0) load_step(3) load_y(3) quantise(3,0,1) quantise(3,0,0)
    multiply(2,1) lay_words(14) turn_back(5,0,1) make_kept(6,0) turn_x(3,0,3,0) finish(5,1) finish(5,0) store(5)
    make_w(7) empty(2,0) empty(2,1) turn_back(6,1,1) mask(6,1) centre(3,0,3) make_kept(7,1) turn_step(2,2)
    copy_step(2,2) turn_x(3,0,2,0) centre(3,0,2) multiply(2,2) quantise(3,0,3) quantise(3,0,2) multiply(2,3)
    lay_words(15) turn_back(6,0,1) make_kept(7,0) turn_x(3,1,1,0) finish(6,1) finish(6,0) store(6) make_w(8)
    empty(2,2) empty(2,3) turn_back(7,1,1) mask(7,1) centre(3,1,1) make_kept(8,1) turn_step(2,4) copy_step(2,4)
    turn_x(3,1,0,0) centre(3,1,0) multiply(2,4) quantise(3,1,1) quantise(3,1,0) multiply(2,5) turn_back(7,0,1)
    make_kept(8,0) turn_x(3,1,3,0) finish(7,1) finish(7,0) store(7) make_w(9) empty(2,4) empty(2,5)
    turn_back(8,1,1) mask(8,1) centre(3,1,3) make_kept(9,1) turn_step(2,6) copy_step(2,6) turn_x(3,1,2,0)
    centre(3,1,2) multiply(2,6) quantise(3,1,3) quantise(3,1,2) multiply(2,7) turn_back(8,0,1) make_kept(9,0)
    finish(8,1) finish(8,0) store(8) make_w(10) make_kept(10,1) turn_back(9,0,0) make_kept(10,0) empty(2,7)
    make_w(11) make_kept(11,1) empty(2,6) turn_back(9,1,1) mask(9,1) finish(9,1) finish(9,0) store(9)
    turn_step(3,0) copy_step(3,0) multiply(3,0) empty(3,0) make_kept(11,0) multiply(3,2) turn_back(10,0,1)
    finish(10,0) turn_back(10,1,1) mask(10,1) finish(10,1) store(10) make_w(12) make_kept(12,0) turn_step(3,2)
    copy_step(3,2) empty(3,2) multiply(3,1) make_kept(12,1) empty(3,1) turn_back(11,1,1) mask(11,1) finish(11,1)
    turn_back(11,0,1) finish(11,0) store(11) multiply(3,3) make_w(13) make_kept(13,0) empty(3,3) multiply(3,4)
    turn_back(12,1,1) mask(12,1) finish(12,1) turn_step(3,4) copy_step(3,4) empty(3,4) make_w(14) multiply(3,7)
    turn_back(13,1,1) mask(13,1) multiply(3,5) turn_back(12,0,1) finish(12,0) store(12) empty(3,7) empty(3,5)
    turn_step(3,6) copy_step(3,6) make_kept(13,1) finish(13,1) turn_back(13,0,1) finish(13,0) store(13)
    multiply(3,6) empty(3,6) turn_back(14,1,1) mask(14,1) turn_back(15,1,1) mask(15,1) make_kept(14,1)
    finish(14,1) turn_back(14,0,1) make_kept(14,0) finish(14,0) store(14) make_w(15) turn_back(15,0,1)
    make_kept(15,0) finish(15,0) make_kept(15,1) finish(15,1) store(15)
"""


def tile_gaussian_imputation_jacobi_s1_kernel(tc, x, mu, pa, pb_words, pb_scales, dinv, y, step, out):
    nc = tc.nc
    with ExitStack() as ctx:
        keep = ctx.enter_context(tc.tile_pool(name="keep", bufs=1))
        work = ctx.enter_context(tc.tile_pool(name="work", bufs=2))
        psum = ctx.enter_context(tc.psum_pool(name="psum", bufs=1))
        ctx.enter_context(nc.allow_non_contiguous_dma(reason="mu lies 4 values a partition"))
        ctx.enter_context(tc.manual_schedule())

        ident_f = keep.tile([P, P], F32, name="ident_f")
        ident_b = keep.tile([P, P], BF16, name="ident_b")
        mu_t = keep.tile([P, PASSES, 4], BF16, name="mu_t", align_bytes=64)
        dinv_rows = keep.tile([P, P], BF16, name="dinv_rows")
        dinv_t = keep.tile([P, BLOCKS], F32, name="dinv_t")
        warm = keep.tile([P, 1], F32, name="warm")
        pa_raw = keep.tile([P, 2, 4, HALF], BF16, name="pa_raw", align_bytes=64)
        pa_grp = keep.tile([P, N, 4], BF16, name="pa_grp", align_bytes=64)
        pa_codes = keep.tile([P, N], U32, name="pa_codes", align_bytes=64)
        pa_scale = keep.tile([P, N], U8, name="pa_scale", align_bytes=64)
        pb_codes = keep.tile([P, PASSES - 1, 2 * N], U8, name="pb_codes", align_bytes=64)
        pb_scale = keep.tile([P, PASSES - 1, N], U8, name="pb_scale", align_bytes=64)

        x_first, x_in, x_words, step_in, y_in = {}, {}, {}, {}, {}
        x_bank, centred, codes, scales = {}, {}, {}, {}
        acc, step_bank, step_t, z, back = {}, {}, {}, {}, {}
        w, kept, result = {}, {}, {}


        def rows_of(ap, group):
            return ap[group * ROWS : (group + 1) * ROWS, :].rearrange("(p i) n -> p i n", i=TILES)

        def load_first(n):
            part, slot = divmod(n, 2)
            if part not in x_first:
                x_first[part] = work.tile([P, 2, TILES, PASS], BF16, name="x_in", tag="x_in", bufs=4, align_bytes=64)
            g = ORDER[n]
            nc.sync.dma_start(
                out=x_first[part][:, slot, :, :],
                in_=rows_of(x, 0)[:, :, g * PASS : (g + 1) * PASS],
            )

        def load_x(pair):
            group, j = divmod(pair, 2)
            x_in[pair] = work.tile([P, 2, K], BF16, name="x_in", tag="x_in", bufs=4, align_bytes=64)
            nc.sync.dma_start(out=x_in[pair][:], in_=rows_of(x, group)[:, 2 * j : 2 * j + 2, :])

        def load_rows(tiles, src, name, group):
            tiles[group] = work.tile([P, TILES, N], BF16, name=name, tag=name, bufs=3, align_bytes=64)
            nc.sync.dma_start(out=tiles[group][:], in_=rows_of(src, group))

        def load_step(group):
            load_rows(step_in, step, "step_in", group)

        def load_first_step(half):
            if 0 not in step_in:
                step_in[0] = work.tile([P, 2, TILES, HALF], BF16, name="step_in", tag="step_in", bufs=3, align_bytes=64)
            cols = slice(half * HALF, (half + 1) * HALF)
            nc.sync.dma_start(out=step_in[0][:, half, :, :], in_=rows_of(step, 0)[:, :, cols])

        def load_y(group):
            load_rows(y_in, y, "y_in", group)

        def step_part(group, half, tiles):
            if group == 0:
                return step_in[0][:, half, tiles, :]
            return step_in[group][:, tiles, half * HALF : (half + 1) * HALF]

        def load_pa(half):
            cols = slice(half * HALF, (half + 1) * HALF)
            nc.sync.dma_start(out=pa_raw[:, half, :, :], in_=pa[:, cols].rearrange("(p t) n -> p t n", t=4))

        def load_pb():
            nc.sync.dma_start(out=pb_codes[:].bitcast(I32), in_=pb_words.rearrange("g p b -> p g b").bitcast(I32))

        def load_pb_scales():
            for q in range(4):
                nc.sync.dma_start(
                    out=pb_scale[32 * q : 32 * q + 4, :, :].bitcast(I32),
                    in_=pb_scales[:, 4 * q : 4 * q + 4, :].rearrange("g r n -> r g n").bitcast(I32),
                )


        def pa_sides(c):
            cols = slice(c * PA_COLS, (c + 1) * PA_COLS)
            half, c = divmod(c, 2)
            source = pa_raw[:, half, :, c * PA_COLS : (c + 1) * PA_COLS]
            return pa_grp[:, cols, :], source.rearrange("p t n -> p n t")

        def lay_pa(c):
            target, source = pa_sides(c)
            nc.scalar.copy(out=target, in_=source)

        def lay_pa_on_vector(c):
            target, source = pa_sides(c)
            nc.vector.tensor_copy(out=target, in_=source)

        def quantise_pa(c):
            cols = slice(c * PA_COLS, (c + 1) * PA_COLS)
            nc.vector.quantize_mx(
                out=pa_codes[:, cols].bitcast(E4M3X4),
                scales=pa_scale[:, cols],
                in_=pa_grp[:, cols, :].rearrange("p n t -> p (n t)"),
            )

        def turn_dinv():
            back["dinv"] = psum.tile([P, P], BF16, name="dinv_bank", tag="step", bufs=1)
            nc.tensor.transpose(back["dinv"][:], dinv_rows[:], ident_b[:])

        def keep_dinv():
            nc.vector.tensor_copy(out=dinv_t[:], in_=back["dinv"][:, 0:BLOCKS])


        def words_of(tile):
            return x_in[tile // 2][:, tile % 2, :].bitcast(F32).rearrange("r (g p u) -> r g u p", p=P, u=2)

        def words_of_pass(tile, g):
            if tile in x_words:
                return x_words[tile][:, g]
            if tile < TILES:
                part, slot = divmod(ORDER.index(g), 2)
                return x_first[part][:, slot, tile, :].bitcast(F32).rearrange("r (p u) -> r u p", u=2)
            return words_of(tile)[:, g]

        def lay_words(tile):
            x_words[tile] = work.tile([P, PASSES, 2, P], F32, name="x_words", tag="x_words", bufs=6, align_bytes=64)
            nc.scalar.copy(out=x_words[tile][:], in_=words_of(tile))

        def turn_x(group, j, g, ring):
            bank = psum.tile([P, 2, PAIR], F32, name="x_bank", tag="ring%d" % ring, bufs=2)
            for i in range(2):
                tile = group * TILES + 2 * j + i
                src = words_of_pass(tile, g)
                for u in range(2):
                    nc.tensor.transpose(bank[:, u, i * P : (i + 1) * P], src[:, u, :], ident_f[:])
            x_bank[(group, j, g)] = bank

        def centre(group, j, g):
            c = work.tile([P, PAIR, 4], BF16, name="centred", tag="centred", bufs=6, align_bytes=64)
            nc.vector.tensor_tensor(
                out=c[:].rearrange("p r (u e) -> p r u e", e=2),
                in0=x_bank[(group, j, g)][:].bitcast(BF16).rearrange("p u (r e) -> p r u e", e=2),
                in1=mu_t[:, g, :].rearrange("p (u e) -> p u e", e=2).unsqueeze(1).to_broadcast([P, PAIR, 2, 2]),
                op=ALU.subtract,
            )
            centred[(group, j, g)] = c

        def quantise(group, j, g):
            if group not in codes:
                codes[group] = work.tile([P, PASSES, ROWS], U32, name="codes", tag="codes", bufs=2, align_bytes=64)
                scales[group] = work.tile([P, PASSES, ROWS], U8, name="scales", tag="scales", bufs=2, align_bytes=64)
            rows = slice(j * PAIR, (j + 1) * PAIR)
            nc.vector.quantize_mx(
                out=codes[group][:, g, rows].bitcast(E4M3X4),
                scales=scales[group][:, g, rows],
                in_=centred[(group, j, g)][:].rearrange("p r t -> p (r t)"),
            )


        def multiply_pass(group, b, g):
            cols = slice(b * P, (b + 1) * P)
            if g == ORDER[0]:
                acc[(group, b)] = psum.tile([P, ROWS], F32, name="acc", tag="acc", bufs=3)
            if g == 0:
                weight, weight_scale = pa_codes[:, cols].bitcast(E4M3X4), pa_scale[:, cols]
            else:
                weight = pb_codes[:, g - 1, 2 * b * P : 2 * (b + 1) * P].bitcast(E2M1X4)
                weight_scale = pb_scale[:, g - 1, cols]
            nc.tensor.matmul_mx(
                out=acc[(group, b)][:],
                lhsT=weight,
                lhsT_scale=weight_scale,
                rhs=codes[group][:, g, :].bitcast(E4M3X4),
                rhs_scale=scales[group][:, g, :],
                start=(g == ORDER[0]),
                stop=(g == ORDER[-1]),
            )

        def multiply(group, b):
            for g in ORDER:
                multiply_pass(group, b, g)

        def turn_step(group, b):
            bank = psum.tile([P, ROWS], BF16, name="step_bank", tag="step", bufs=1)
            cols = slice(b % 4 * P, (b % 4 + 1) * P)
            for i in range(TILES):
                nc.tensor.transpose(bank[:, i * P : (i + 1) * P], step_part(group, b // 4, i)[:, cols], ident_b[:])
            step_bank[(group, b)] = bank

        def copy_step(group, b):
            step_t[(group, b)] = work.tile([P, ROWS], BF16, name="step_t", tag="step_t", bufs=3, align_bytes=64)
            nc.scalar.copy(out=step_t[(group, b)][:], in_=step_bank[(group, b)][:])

        def masked_before(group, b):
            return b % 2 in MASKED_BEFORE[group]

        def empty(group, b):
            z[(group, b)] = work.tile([P, ROWS], F32, name="z", tag="z", bufs=12, align_bytes=64)
            if masked_before(group, b):
                nc.vector.scalar_tensor_tensor(
                    out=z[(group, b)][:],
                    in0=acc[(group, b)][:],
                    scalar=dinv_t[:, b : b + 1],
                    in1=step_t[(group, b)][:],
                    op0=ALU.mult,
                    op1=ALU.mult,
                )
            else:
                nc.scalar.activation(
                    out=z[(group, b)][:],
                    in_=acc[(group, b)][:],
                    func=ACT.Identity,
                    bias=0.0,
                    scale=dinv_t[:, b : b + 1],
                )


        def place(m):
            group, q = divmod(m, 4)
            half, j = divmod(q, 2)
            return group, half, slice(2 * j, 2 * j + 2), slice(half * HALF, (half + 1) * HALF)

        def every_2nd(ap, odd):
            return ap.rearrange("p i (c k n) -> p k i c n", k=2, n=P)[:, odd]

        def turn_back(m, odd, ring):
            group, half, tiles, cols = place(m)
            bank = psum.tile([P, 2, 2, P], F32, name="back", tag="ring%d" % ring, bufs=2)
            for i in range(2):
                for c in range(2):
                    src = z[(group, 4 * half + 2 * c + odd)]
                    rows = slice((tiles.start + i) * P, (tiles.start + i + 1) * P)
                    nc.tensor.transpose(bank[:, i, c, :], src[:, rows], ident_f[:])
            back[(m, odd)] = bank

        def make_w(m):
            group, half, tiles, cols = place(m)
            w[m] = work.tile([P, 2, HALF], F32, name="w", tag="w", bufs=2, align_bytes=64)
            nc.scalar.activation(out=w[m][:], in_=step_part(group, half, tiles), func=ACT.Identity, bias=1.0, scale=-1.0)

        def multiply_kept(engine, m, odd):
            group, half, tiles, cols = place(m)
            name = "kept%d" % odd
            kept[(m, odd)] = work.tile([P, 2, 2, P], F32, name=name, tag=name, bufs=2, align_bytes=64)
            engine.tensor_tensor(
                out=kept[(m, odd)][:],
                in0=every_2nd(w[m][:], odd),
                in1=every_2nd(y_in[group][:, tiles, cols], odd),
                op=ALU.mult,
            )

        def make_kept(m, odd):
            multiply_kept(nc.gpsimd, m, odd)

        def make_kept_on_vector(m, odd):
            multiply_kept(nc.vector, m, odd)

        def mask(m, odd):
            group, half, tiles, cols = place(m)
            t = work.tile([P, 2, 2, P], F32, name="masked", tag="masked", bufs=2, align_bytes=64)
            nc.vector.tensor_tensor(
                out=t[:], in0=back[(m, odd)][:], in1=every_2nd(step_part(group, half, tiles), odd), op=ALU.mult
            )
            back[(m, odd)] = t

        def subtract(m, odd, i):
            nc.vector.tensor_tensor(
                out=every_2nd(result[m][:], odd)[:, i],
                in0=kept[(m, odd)][:, i],
                in1=back[(m, odd)][:, i],
                op=ALU.subtract,
            )

        def finish(m, odd):
            if m not in result:
                result[m] = work.tile([P, 2, HALF], F32, name="result", tag="result", bufs=3, align_bytes=64)
            subtract(m, odd, slice(0, 2))

        def finish_and_store(m, odd):
            group, half, tiles, cols = place(m)
            for i in range(2):
                subtract(m, odd, i)
                nc.sync.dma_start(out=rows_of(out, group)[:, tiles.start + i, cols], in_=result[m][:, i, :])

        def store(m):
            group, half, tiles, cols = place(m)
            nc.sync.dma_start(out=rows_of(out, group)[:, tiles, cols], in_=result[m][:])

        nc.scalar.dma_start(out=mu_t[:], in_=mu.rearrange("(g p t) -> p g t", p=P, t=4))
        nc.vector.memset(dinv_rows[:], 0.0)
        nc.scalar.dma_start(out=dinv_rows[0:BLOCKS, :], in_=dinv.rearrange("(b p) -> b p", p=P))
        nc.vector.memset(warm[:], 0.0)
        nc.scalar.activation(out=warm[:], in_=warm[:], func=ACT.Identity, bias=0.0, scale=1.0)
        nc.vector.memset(pb_scale[:].rearrange("p g n -> p (g n)").bitcast(I32), 0)
        make_identity(nc, ident_f[:])
        make_identity(nc, ident_b[:])

        call = dict(
            load_first=load_first, load_x=load_x, load_step=load_step, load_first_step=load_first_step, load_y=load_y, load_pa=load_pa, load_pb=load_pb,
            load_pb_scales=load_pb_scales, lay_pa=lay_pa, lay_pa_on_vector=lay_pa_on_vector, quantise_pa=quantise_pa,
            turn_dinv=turn_dinv, keep_dinv=keep_dinv, lay_words=lay_words, turn_x=turn_x, centre=centre,
            quantise=quantise, multiply_pass=multiply_pass, multiply=multiply, turn_step=turn_step,
            copy_step=copy_step, empty=empty, turn_back=turn_back, make_w=make_w, make_kept=make_kept,
            make_kept_on_vector=make_kept_on_vector, mask=mask, finish=finish, finish_and_store=finish_and_store, store=store,
        )
        for text in CALLS.split():
            name, numbers = text.replace(")", "").split("(")
            call[name](*[int(number) for number in numbers.split(",") if number])
